import numpy as np
import ml_dtypes


def mxq(x, axis, fmt="e4m3"):
    dtype, down = {"e4m3": (ml_dtypes.float8_e4m3fn, 7), "e5m2": (ml_dtypes.float8_e5m2, 14)}[fmt]
    v = np.moveaxis(np.asarray(x, np.float32).astype(ml_dtypes.bfloat16).astype(np.float64), axis, -1)
    blocks = v.reshape(v.shape[:-1] + (-1, 32))
    amax = np.abs(blocks).max(-1, keepdims=True)
    byte = np.maximum(np.where(amax > 0, np.frexp(amax)[1] - 1 + 127, 0) - down, 1)
    scale = np.exp2(byte - 127.0)
    codes = (blocks / scale).astype(np.float32).astype(dtype).astype(np.float64)
    return np.moveaxis((codes * scale).reshape(v.shape), -1, axis)


WIDE = False


def mx_kscale(k):
    if not WIDE:
        return np.ones(k)
    levels = np.array([10, -10, 5, -5, 0])
    if k % 512:
        return np.exp2(np.random.permutation(np.resize(levels, k // 32))).repeat(32)
    a = np.empty((k // 512, 16))
    for p in range(k // 512):
        a[p, :8] = np.random.permutation(np.resize(levels, 8))
        for g in range(8):
            far = levels[np.abs(levels - a[p, g]) >= 10]
            a[p, g + 8] = far[np.random.randint(len(far))]
    return np.exp2(a.ravel()).repeat(32)


def f64(x):
    return np.asarray(x).astype(np.float64)


def striped(idx):
    return np.tile(idx.reshape(-1, 16).T, (8, 1)).astype(np.uint16)


def unstriped(offs):
    return offs[:16].T.reshape(-1).astype(np.int64)


def pack_weight(w):
    k, n = w.shape
    w = f64(np.asarray(w, np.float32).astype(ml_dtypes.bfloat16)).reshape(k // 32, 32, n)
    amax = np.abs(w).max(1)
    byte = np.clip(np.where(amax > 0, np.frexp(amax)[1] - 1 + 127 - 7, 1), 1, 254)
    scaled = (w * np.exp2(127.0 - byte)[:, None, :]).reshape(k, n).astype(np.float32)
    words = np.ascontiguousarray(scaled.reshape(k // 512, 128, 4, n).transpose(0, 1, 3, 2)).astype(ml_dtypes.float8_e4m3fn).view(np.uint8)
    return words, np.ascontiguousarray(byte.astype(np.uint8).reshape(k // 512, 16, n))


def unpack_weight(words, scales):
    g, p, n, _ = words.shape
    vals = np.ascontiguousarray(words).view(ml_dtypes.float8_e4m3fn).astype(np.float64) * np.repeat(np.exp2(scales.astype(np.float64) - 127.0), 8, axis=1)[..., None]
    return vals.transpose(0, 1, 3, 2).reshape(g * 512, n)


def sigmoid(v):
    return 1.0 / (1.0 + np.exp(-np.maximum(v, -700.0)))


K, T, S, D, H, G, R = 512, 1024, 512, 8, 512, 2048, 512
P = 2 ** 7


def setup_inputs():
    n = np.random.standard_normal
    s = mx_kscale(K)[:, None]
    u = mx_kscale(H)
    packed_xT = pack_weight(n((K, T)) * s)
    packed_vT = pack_weight(n((H, G)) / np.sqrt(H) / u[:, None])
    return {
        "x_words": packed_xT[0],
        "x_scales": packed_xT[1],
        "w1": (n((K, H)) / np.sqrt(K) / s * u).astype(np.float32),
        "norm": (np.tile(np.random.uniform(0.3, 0.7, S), (P, 1))).astype(np.float32),
        "v_words": packed_vT[0],
        "v_scales": packed_vT[1],
        "bias": (np.tile(0.5 * n(G), (P, 1))).astype(np.float32),
        "offs": striped(np.random.permutation(T)[:S]),
        "items": striped(np.random.permutation(G)[:R]),
    }


def reference(x_words, x_scales, w1, norm, v_words, v_scales, bias, offs, items):
    xq = unpack_weight(x_words, x_scales)[:, unstriped(offs)]
    y = mxq(f64(w1), 0, "e4m3").T @ xq
    ss = y.reshape(len(y), -1, D).sum(axis=2)
    z = (np.repeat(ss, D, axis=1) - y) * f64(norm)[:1]
    v_items = unpack_weight(v_words, v_scales)[:, unstriped(items)]
    sc = mxq(z, 0, "e4m3").T @ v_items
    return sigmoid(sc + f64(bias)[:1][:, unstriped(items)])

@@ -1,0 +1,211 @@
+from contextlib import ExitStack
+
+import concourse.mybir as mybir
+from concourse.masks import make_identity
+
+K, T, S, D, H, G, R = 512, 1024, 512, 8, 512, 2048, 512
+FLOPS = 2 * K * H * S + 2 * H * S * R
+
+F32 = mybir.dt.float32
+BF16 = mybir.dt.bfloat16
+I32 = mybir.dt.int32
+U32 = mybir.dt.uint32
+U16 = mybir.dt.uint16
+U8 = mybir.dt.uint8
+FP8X4 = mybir.dt.float8_e4m3fn_x4
+ALU = mybir.AluOpType
+ACT = mybir.ActivationFunctionType
+AX = mybir.AxisListType
+
+P = 128
+PACK = 4
+TILES = S // P
+BASKETS = P // D
+
+
+def load_scale_rows(queue, plane, rows):
+    for q in range(4):
+        queue.dma_start(out=plane[32 * q : 32 * q + 4, :].bitcast(I32), in_=rows[0, 4 * q : 4 * q + 4, :].bitcast(I32))
+
+
+def tile_picked_yfism_sig_p_kernel(
+    tc, x_words, x_scales, w1, norm, v_words, v_scales, bias, offs, items, out
+):
+    nc = tc.nc
+    with ExitStack() as ctx:
+        keep = ctx.enter_context(tc.tile_pool(name="keep", bufs=1))
+        ring = ctx.enter_context(tc.tile_pool(name="ring", bufs=5))
+        psum_y = ctx.enter_context(tc.psum_pool(name="psum_y", bufs=4))
+        psum_s = ctx.enter_context(tc.psum_pool(name="psum_s", bufs=2))
+        psum_o = ctx.enter_context(tc.psum_pool(name="psum_o", bufs=2))
+
+        offs_sb = keep.tile([P, S // 16], U16, name="offs_sb")
+        items_sb = keep.tile([P, R // 16], U16, name="items_sb")
+        x_table = keep.tile([P, T], U32, name="x_table", align_bytes=64)
+        x_table_scales = keep.tile([P, T], U8, name="x_table_scales", align_bytes=64)
+        v_table = keep.tile([P, G], U32, name="v_table", align_bytes=64)
+        v_table_scales = keep.tile([P, G], U8, name="v_table_scales", align_bytes=64)
+        bias_table = keep.tile([P, G], F32, name="bias_table", align_bytes=64)
+        norm_sb = keep.tile([P, S], F32, name="norm_sb", align_bytes=64)
+        half = H // 2
+        w_raw = [keep.tile([P, PACK, half], F32, name="w_raw%d" % a, align_bytes=64) for a in range(2)]
+        ident = keep.tile([P, P], F32, name="ident", align_bytes=64)
+        warm_in = keep.tile([P, 1], F32, name="warm_in")
+        warm_out = keep.tile([P, 1], F32, name="warm_out")
+
+        nc.vector.memset(x_table_scales[:].bitcast(I32), 0)
+        nc.gpsimd.memset(warm_in[:], 0.0)
+        nc.scalar.activation(warm_out[:], warm_in[:], ACT.Sigmoid)
+        nc.vector.memset(v_table_scales[:].bitcast(I32), 0)
+        nc.gpsimd.memset(bias_table[:], 0.0)
+
+        nc.sync.dma_start(offs_sb[:], offs)
+        nc.sync.dma_start(out=x_table[:].bitcast(I32), in_=x_words[0].rearrange("p n r -> p (n r)").bitcast(I32))
+        load_scale_rows(nc.scalar, x_table_scales, x_scales)
+        w_rows = w1.rearrange("(p r) c -> p r c", r=PACK)
+        for a in range(2):
+            nc.sync.dma_start(out=w_raw[a][:], in_=w_rows[:, :, a * half : (a + 1) * half])
+        nc.sync.dma_start(items_sb[:], items)
+        nc.sync.dma_start(out=bias_table[0:1, :], in_=bias[0:1, :])
+        nc.sync.dma_start(out=norm_sb[:], in_=norm)
+        nc.sync.dma_start(out=v_table[:].bitcast(I32), in_=v_words[0].rearrange("p n r -> p (n r)").bitcast(I32))
+        load_scale_rows(nc.sync, v_table_scales, v_scales)
+        make_identity(nc, ident[:])
+
+        x_codes = keep.tile([P, S], U32, name="x_codes", align_bytes=64)
+        x_plane = keep.tile([P, S], U8, name="x_plane", align_bytes=64)
+        nc.vector.tensor_copy(x_codes[:], x_table[:].indirect(offs_sb[:]))
+        nc.vector.tensor_copy(x_plane[:], x_table_scales[:].indirect(offs_sb[:]))
+
+        w_grouped = keep.tile([P, PACK, P, PACK], BF16, name="w_grouped", align_bytes=64)
+        for a in range(2):
+            nc.scalar.copy(
+                w_grouped[:, :, a * (P // 2) : (a + 1) * (P // 2), :].rearrange("p j m r -> p m j r"),
+                w_raw[a][:].rearrange("p r (m j) -> p m j r", j=PACK),
+            )
+        w_codes = keep.tile([P, PACK, P], U32, name="w_codes", align_bytes=64)
+        w_plane = keep.tile([P, PACK, P], U8, name="w_plane", align_bytes=64)
+        for j in range(PACK):
+            nc.vector.quantize_mx(
+                out=w_codes[:, j, :].bitcast(FP8X4),
+                scales=w_plane[:, j, :],
+                in_=w_grouped[:, j, :, :].rearrange("p m r -> p (m r)"),
+            )
+
+        y_banks = []
+        for a in range(TILES):
+            cols = slice(a * P, (a + 1) * P)
+            y = psum_y.tile([P, PACK, P], F32, name="y")
+            for j in range(PACK):
+                nc.tensor.matmul_mx(
+                    out=y[:, j, :],
+                    lhsT=w_codes[:, j, :].bitcast(FP8X4),
+                    lhsT_scale=w_plane[:, j, :],
+                    rhs=x_codes[:, cols].bitcast(FP8X4),
+                    rhs_scale=x_plane[:, cols],
+                    start=True,
+                    stop=True,
+                )
+            y_banks.append(y)
+
+        bias_picked = keep.tile([P, R], F32, name="bias_picked", align_bytes=64)
+        nc.vector.tensor_copy(bias_picked[:], bias_table[:].indirect(items_sb[:]))
+        bias_turned = psum_o.tile([P, TILES, P], F32, name="turned")
+        for b in range(TILES):
+            nc.tensor.transpose(bias_turned[:, b, :], bias_picked[:, b * P : (b + 1) * P], ident[:])
+        bias_cols = keep.tile([P, TILES], F32, name="bias_cols")
+        nc.scalar.copy(bias_cols[:], bias_turned[:, :, 0])
+        bias_spread = psum_o.tile([P, TILES, P], F32, name="turned")
+        for b in range(TILES):
+            nc.tensor.transpose(bias_spread[:, b, :], bias_cols[:, b : b + 1].to_broadcast([P, P]), ident[:])
+        bias_rows = keep.tile([P, R], F32, name="bias_rows", align_bytes=64)
+        nc.scalar.copy(bias_rows[:], bias_spread[:].rearrange("p b g -> p (b g)"))
+
+        v_codes = keep.tile([P, R], U32, name="v_codes", align_bytes=64)
+        v_plane = keep.tile([P, R], U8, name="v_plane", align_bytes=64)
+
+        z_bf = {}
+
+        def leave_one_out(a):
+            y = y_banks[a]
+            sums = ring.tile([P, BASKETS, PACK], F32, name="sums", align_bytes=64)
+            nc.vector.tensor_reduce(sums[:], y[:].rearrange("p j (v d) -> p v j d", d=D), AX.X, ALU.add)
+            others = ring.tile([P, BASKETS, D, PACK], F32, name="others", align_bytes=64)
+            nc.vector.tensor_tensor(
+                others[:],
+                sums[:].unsqueeze(2).to_broadcast([P, BASKETS, D, PACK]),
+                y[:].rearrange("p j (v d) -> p v d j", d=D),
+                ALU.subtract,
+            )
+            z = ring.tile([P, P, PACK], BF16, name="z", align_bytes=64)
+            nc.gpsimd.tensor_tensor(
+                z[:],
+                others[:].rearrange("p v d j -> p (v d) j"),
+                norm_sb[:, a * P : (a + 1) * P].unsqueeze(2).to_broadcast([P, P, PACK]),
+                ALU.mult,
+            )
+            z_bf[a] = z
+
+        def quantize_z(a):
+            z_codes = ring.tile([P, P], U32, name="z_codes", align_bytes=64)
+            z_plane = ring.tile([P, P], U8, name="z_plane", align_bytes=64)
+            nc.vector.quantize_mx(
+                out=z_codes[:].bitcast(FP8X4), scales=z_plane[:], in_=z_bf[a][:].rearrange("p t j -> p (t j)")
+            )
+            return z_codes, z_plane
+
+        def score_direct(a, parts, pool, tag):
+            z_codes, z_plane = quantize_z(a)
+            width = R // parts
+            for c in range(parts):
+                cols = slice(c * width, (c + 1) * width)
+                sc = pool.tile([P, width], F32, name=tag)
+                nc.tensor.matmul_mx(
+                    out=sc[:],
+                    lhsT=z_codes[:].bitcast(FP8X4),
+                    lhsT_scale=z_plane[:],
+                    rhs=v_codes[:, cols].bitcast(FP8X4),
+                    rhs_scale=v_plane[:, cols],
+                    start=True,
+                    stop=True,
+                )
+                logits = ring.tile([P, width], F32, name="logits", align_bytes=64)
+                nc.vector.tensor_tensor(logits[:], sc[:], bias_rows[:, cols], ALU.add)
+                result = ring.tile([P, width], F32, name="result", align_bytes=64)
+                nc.scalar.activation(result[:], logits[:], ACT.Sigmoid)
+                nc.sync.dma_start(out=out[a * P : (a + 1) * P, cols], in_=result[:])
+
+        def score_turned(a):
+            z_codes, z_plane = quantize_z(a)
+            sc = psum_s.tile([P, TILES, P], F32, name="sc")
+            for b in range(TILES):
+                cols = slice(b * P, (b + 1) * P)
+                nc.tensor.matmul_mx(
+                    out=sc[:, b, :],
+                    lhsT=v_codes[:, cols].bitcast(FP8X4),
+                    lhsT_scale=v_plane[:, cols],
+                    rhs=z_codes[:].bitcast(FP8X4),
+                    rhs_scale=z_plane[:],
+                    start=True,
+                    stop=True,
+                )
+            probs = ring.tile([P, TILES, P], F32, name="probs", align_bytes=64)
+            for b in range(TILES):
+                nc.scalar.activation(probs[:, b, :], sc[:, b, :], ACT.Sigmoid, bias=bias_cols[:, b : b + 1])
+            turned = psum_o.tile([P, TILES, P], F32, name="turned")
+            for b in range(TILES):
+                nc.tensor.transpose(turned[:, b, :], probs[:, b, :], ident[:])
+            result = ring.tile([P, R], F32, name="result", align_bytes=64)
+            nc.scalar.copy(result[:], turned[:].rearrange("p b g -> p (b g)"))
+            nc.sync.dma_start(out=out[a * P : (a + 1) * P, :], in_=result[:])
+
+        nc.vector.tensor_copy(v_plane[:], v_table_scales[:].indirect(items_sb[:]))
+        leave_one_out(0)
+        nc.vector.tensor_copy(v_codes[:], v_table[:].indirect(items_sb[:]))
+        leave_one_out(1)
+        score_turned(0)
+        leave_one_out(2)
+        score_turned(1)
+        leave_one_out(3)
+        score_direct(2, 1, psum_s, "sc")
+        score_direct(3, 2, psum_o, "turned")

@@ -21,6 +21,7 @@ P = 128
 PACK = 4
 TILES = S // P
 BASKETS = P // D
+CAST_SPLIT = 44
 
 
 def load_scale_rows(queue, plane, rows):
@@ -35,16 +36,16 @@ def tile_picked_yfism_sig_p_kernel(
     with ExitStack() as ctx:
         keep = ctx.enter_context(tc.tile_pool(name="keep", bufs=1))
         ring = ctx.enter_context(tc.tile_pool(name="ring", bufs=5))
-        psum_y = ctx.enter_context(tc.psum_pool(name="psum_y", bufs=4))
+        psum_y = ctx.enter_context(tc.psum_pool(name="psum_y", bufs=3))
         psum_s = ctx.enter_context(tc.psum_pool(name="psum_s", bufs=2))
-        psum_o = ctx.enter_context(tc.psum_pool(name="psum_o", bufs=2))
+        psum_o = ctx.enter_context(tc.psum_pool(name="psum_o", bufs=3))
 
         offs_sb = keep.tile([P, S // 16], U16, name="offs_sb")
         items_sb = keep.tile([P, R // 16], U16, name="items_sb")
         x_table = keep.tile([P, T], U32, name="x_table", align_bytes=64)
         x_table_scales = keep.tile([P, T], U8, name="x_table_scales", align_bytes=64)
         v_table = keep.tile([P, G], U32, name="v_table", align_bytes=64)
-        v_table_scales = keep.tile([P, G], U8, name="v_table_scales", align_bytes=64)
+        v_table_scales = keep.tile([P, G], U8, name="v_table_scales", tag="scales_then_others", align_bytes=64)
         bias_table = keep.tile([P, G], F32, name="bias_table", align_bytes=64)
         norm_sb = keep.tile([P, S], F32, name="norm_sb", align_bytes=64)
         half = H // 2
@@ -53,22 +54,22 @@ def tile_picked_yfism_sig_p_kernel(
         warm_in = keep.tile([P, 1], F32, name="warm_in")
         warm_out = keep.tile([P, 1], F32, name="warm_out")
 
-        nc.vector.memset(x_table_scales[:].bitcast(I32), 0)
+        nc.gpsimd.memset(x_table_scales[:].bitcast(I32), 0)
         nc.gpsimd.memset(warm_in[:], 0.0)
         nc.scalar.activation(warm_out[:], warm_in[:], ACT.Sigmoid)
-        nc.vector.memset(v_table_scales[:].bitcast(I32), 0)
-        nc.gpsimd.memset(bias_table[:], 0.0)
+        nc.gpsimd.memset(v_table_scales[:].bitcast(I32), 0)
+        nc.vector.memset(bias_table[:], 0.0)
 
+        w_rows = w1.rearrange("(p r) c -> p r c", r=PACK)
         nc.sync.dma_start(offs_sb[:], offs)
         nc.sync.dma_start(out=x_table[:].bitcast(I32), in_=x_words[0].rearrange("p n r -> p (n r)").bitcast(I32))
-        load_scale_rows(nc.scalar, x_table_scales, x_scales)
-        w_rows = w1.rearrange("(p r) c -> p r c", r=PACK)
+        load_scale_rows(nc.sync, x_table_scales, x_scales)
         for a in range(2):
             nc.sync.dma_start(out=w_raw[a][:], in_=w_rows[:, :, a * half : (a + 1) * half])
         nc.sync.dma_start(items_sb[:], items)
         nc.sync.dma_start(out=bias_table[0:1, :], in_=bias[0:1, :])
-        nc.sync.dma_start(out=norm_sb[:], in_=norm)
         nc.sync.dma_start(out=v_table[:].bitcast(I32), in_=v_words[0].rearrange("p n r -> p (n r)").bitcast(I32))
+        nc.sync.dma_start(out=norm_sb[:], in_=norm)
         load_scale_rows(nc.sync, v_table_scales, v_scales)
         make_identity(nc, ident[:])
 
@@ -77,11 +78,17 @@ def tile_picked_yfism_sig_p_kernel(
         nc.vector.tensor_copy(x_codes[:], x_table[:].indirect(offs_sb[:]))
         nc.vector.tensor_copy(x_plane[:], x_table_scales[:].indirect(offs_sb[:]))
 
+
         w_grouped = keep.tile([P, PACK, P, PACK], BF16, name="w_grouped", align_bytes=64)
-        for a in range(2):
-            nc.scalar.copy(
-                w_grouped[:, :, a * (P // 2) : (a + 1) * (P // 2), :].rearrange("p j m r -> p m j r"),
-                w_raw[a][:].rearrange("p r (m j) -> p m j r", j=PACK),
+        rows = P // 2
+        for copy, a, lo, hi in (
+            (nc.scalar.copy, 0, 0, rows),
+            (nc.vector.tensor_copy, 1, 0, CAST_SPLIT),
+            (nc.scalar.copy, 1, CAST_SPLIT, rows),
+        ):
+            copy(
+                w_grouped[:, :, a * rows + lo : a * rows + hi, :].rearrange("p j m r -> p m j r"),
+                w_raw[a][:].rearrange("p r (m j) -> p m j r", j=PACK)[:, lo:hi],
             )
         w_codes = keep.tile([P, PACK, P], U32, name="w_codes", align_bytes=64)
         w_plane = keep.tile([P, PACK, P], U8, name="w_plane", align_bytes=64)
@@ -92,13 +99,18 @@ def tile_picked_yfism_sig_p_kernel(
                 in_=w_grouped[:, j, :, :].rearrange("p m r -> p (m r)"),
             )
 
-        y_banks = []
-        for a in range(TILES):
+        v_codes = keep.tile([P, R], U32, name="v_codes", align_bytes=64)
+        v_plane = keep.tile([P, R], U8, name="v_plane", align_bytes=64)
+
+        sums, z_bf, z_mx, y_banks = {}, {}, {}, {}
+        y_sb = [keep.tile([P, D, 2, BASKETS, PACK], F32, name="y_sb%d" % s, align_bytes=64) for s in range(2)]
+
+        def project(a):
             cols = slice(a * P, (a + 1) * P)
-            y = psum_y.tile([P, PACK, P], F32, name="y")
+            y_banks[a] = psum_y.tile([P, PACK, P], F32, name="y")
             for j in range(PACK):
                 nc.tensor.matmul_mx(
-                    out=y[:, j, :],
+                    out=y_banks[a][:, j, :],
                     lhsT=w_codes[:, j, :].bitcast(FP8X4),
                     lhsT_scale=w_plane[:, j, :],
                     rhs=x_codes[:, cols].bitcast(FP8X4),
@@ -106,45 +118,42 @@ def tile_picked_yfism_sig_p_kernel(
                     start=True,
                     stop=True,
                 )
-            y_banks.append(y)
+            pair, side = divmod(a, 2)
+            nc.scalar.copy(y_sb[pair][:, :, side], y_banks[a][:].rearrange("p j (v d) -> p d v j", d=D))
 
-        bias_picked = keep.tile([P, R], F32, name="bias_picked", align_bytes=64)
-        nc.vector.tensor_copy(bias_picked[:], bias_table[:].indirect(items_sb[:]))
-        bias_turned = psum_o.tile([P, TILES, P], F32, name="turned")
-        for b in range(TILES):
-            nc.tensor.transpose(bias_turned[:, b, :], bias_picked[:, b * P : (b + 1) * P], ident[:])
-        bias_cols = keep.tile([P, TILES], F32, name="bias_cols")
-        nc.scalar.copy(bias_cols[:], bias_turned[:, :, 0])
-        bias_spread = psum_o.tile([P, TILES, P], F32, name="turned")
-        for b in range(TILES):
-            nc.tensor.transpose(bias_spread[:, b, :], bias_cols[:, b : b + 1].to_broadcast([P, P]), ident[:])
-        bias_rows = keep.tile([P, R], F32, name="bias_rows", align_bytes=64)
-        nc.scalar.copy(bias_rows[:], bias_spread[:].rearrange("p b g -> p (b g)"))
+        def basket_sums(pair):
+            turned = psum_o.tile([P, P], F32, name="turned")
+            for d in range(D):
+                nc.tensor.matmul(
+                    turned[:],
+                    lhsT=y_sb[pair][:, d].rearrange("p s v j -> p (s v j)"),
+                    rhs=ident[:],
+                    start=(d == 0),
+                    stop=(d == D - 1),
+                    is_transpose=True,
+                )
+            turned_sb = ring.tile([P, P], F32, name="turned_sb", align_bytes=64)
+            nc.scalar.copy(turned_sb[:], turned[:])
+            sums[pair] = psum_s.tile([P, 2, BASKETS, PACK], F32, name="sums")
+            nc.tensor.transpose(sums[pair][:].rearrange("p s v j -> p (s v j)"), turned_sb[:], ident[:])
 
-        v_codes = keep.tile([P, R], U32, name="v_codes", align_bytes=64)
-        v_plane = keep.tile([P, R], U8, name="v_plane", align_bytes=64)
-
-        z_bf = {}
-
-        def leave_one_out(a):
-            y = y_banks[a]
-            sums = ring.tile([P, BASKETS, PACK], F32, name="sums", align_bytes=64)
-            nc.vector.tensor_reduce(sums[:], y[:].rearrange("p j (v d) -> p v j d", d=D), AX.X, ALU.add)
-            others = ring.tile([P, BASKETS, D, PACK], F32, name="others", align_bytes=64)
+        def leave_out(a):
+            pair, side = divmod(a, 2)
             nc.vector.tensor_tensor(
-                others[:],
-                sums[:].unsqueeze(2).to_broadcast([P, BASKETS, D, PACK]),
-                y[:].rearrange("p j (v d) -> p v d j", d=D),
+                others[:, a],
+                sums[pair][:, side].unsqueeze(2).to_broadcast([P, BASKETS, D, PACK]),
+                y_sb[pair][:, :, side].rearrange("p d v j -> p v d j"),
                 ALU.subtract,
             )
-            z = ring.tile([P, P, PACK], BF16, name="z", align_bytes=64)
-            nc.gpsimd.tensor_tensor(
-                z[:],
-                others[:].rearrange("p v d j -> p (v d) j"),
+
+        def scale_by_norm(a):
+            z_bf[a] = ring.tile([P, P, PACK], BF16, name="z", align_bytes=64)
+            nc.vector.tensor_tensor(
+                z_bf[a][:],
+                others[:, a].rearrange("p v d j -> p (v d) j"),
                 norm_sb[:, a * P : (a + 1) * P].unsqueeze(2).to_broadcast([P, P, PACK]),
                 ALU.mult,
             )
-            z_bf[a] = z
 
         def quantize_z(a):
             z_codes = ring.tile([P, P], U32, name="z_codes", align_bytes=64)
@@ -152,16 +161,16 @@ def tile_picked_yfism_sig_p_kernel(
             nc.vector.quantize_mx(
                 out=z_codes[:].bitcast(FP8X4), scales=z_plane[:], in_=z_bf[a][:].rearrange("p t j -> p (t j)")
             )
-            return z_codes, z_plane
+            z_mx[a] = (z_codes, z_plane)
 
         def score_direct(a, parts, pool, tag):
-            z_codes, z_plane = quantize_z(a)
+            z_codes, z_plane = z_mx[a]
             width = R // parts
+            sc = pool.tile([P, R], F32, name=tag)
             for c in range(parts):
                 cols = slice(c * width, (c + 1) * width)
-                sc = pool.tile([P, width], F32, name=tag)
                 nc.tensor.matmul_mx(
-                    out=sc[:],
+                    out=sc[:, cols],
                     lhsT=z_codes[:].bitcast(FP8X4),
                     lhsT_scale=z_plane[:],
                     rhs=v_codes[:, cols].bitcast(FP8X4),
@@ -169,15 +178,17 @@ def tile_picked_yfism_sig_p_kernel(
                     start=True,
                     stop=True,
                 )
+            for c in range(parts):
+                cols = slice(c * width, (c + 1) * width)
                 logits = ring.tile([P, width], F32, name="logits", align_bytes=64)
-                nc.vector.tensor_tensor(logits[:], sc[:], bias_rows[:, cols], ALU.add)
+                nc.vector.tensor_tensor(logits[:], sc[:, cols], bias_rows[:, cols], ALU.add)
                 result = ring.tile([P, width], F32, name="result", align_bytes=64)
                 nc.scalar.activation(result[:], logits[:], ACT.Sigmoid)
                 nc.sync.dma_start(out=out[a * P : (a + 1) * P, cols], in_=result[:])
 
         def score_turned(a):
-            z_codes, z_plane = quantize_z(a)
-            sc = psum_s.tile([P, TILES, P], F32, name="sc")
+            z_codes, z_plane = z_mx[a]
+            sc = psum_y.tile([P, TILES, P], F32, name="y")
             for b in range(TILES):
                 cols = slice(b * P, (b + 1) * P)
                 nc.tensor.matmul_mx(
@@ -199,13 +210,41 @@ def tile_picked_yfism_sig_p_kernel(
             nc.scalar.copy(result[:], turned[:].rearrange("p b g -> p (b g)"))
             nc.sync.dma_start(out=out[a * P : (a + 1) * P, :], in_=result[:])
 
-        nc.vector.tensor_copy(v_plane[:], v_table_scales[:].indirect(items_sb[:]))
-        leave_one_out(0)
+        project(0)
+        project(1)
+        basket_sums(0)
+        project(2)
+        project(3)
+        basket_sums(1)
+        bias_picked = keep.tile([P, R], F32, name="bias_picked", align_bytes=64)
+        nc.vector.tensor_copy(bias_picked[:], bias_table[:].indirect(items_sb[:]))
+        bias_turned = psum_o.tile([P, TILES, P], F32, name="turned")
+        for b in range(TILES):
+            nc.tensor.transpose(bias_turned[:, b, :], bias_picked[:, b * P : (b + 1) * P], ident[:])
+        bias_cols = keep.tile([P, TILES], F32, name="bias_cols")
+        nc.scalar.copy(bias_cols[:], bias_turned[:, :, 0])
+        bias_spread = psum_o.tile([P, TILES, P], F32, name="turned")
+        for b in range(TILES):
+            nc.tensor.transpose(bias_spread[:, b, :], bias_cols[:, b : b + 1].to_broadcast([P, P]), ident[:])
+        bias_rows = keep.tile([P, R], F32, name="bias_rows", align_bytes=64)
+        nc.scalar.copy(bias_rows[:], bias_spread[:].rearrange("p b g -> p (b g)"))
+
         nc.vector.tensor_copy(v_codes[:], v_table[:].indirect(items_sb[:]))
-        leave_one_out(1)
+        nc.vector.tensor_copy(v_plane[:], v_table_scales[:].indirect(items_sb[:]))
+        others = keep.tile([P, TILES, BASKETS, D, PACK], F32, name="others", tag="scales_then_others", align_bytes=64)
+        leave_out(0)
+        leave_out(1)
+        scale_by_norm(0)
+        leave_out(2)
+        quantize_z(0)
         score_turned(0)
-        leave_one_out(2)
+        scale_by_norm(1)
+        scale_by_norm(2)
+        quantize_z(1)
         score_turned(1)
-        leave_one_out(3)
-        score_direct(2, 1, psum_s, "sc")
-        score_direct(3, 2, psum_o, "turned")
+        leave_out(3)
+        quantize_z(2)
+        scale_by_norm(3)
+        quantize_z(3)
+        score_direct(2, 1, psum_s, "sums")
+        score_direct(3, 2, psum_s, "sums")

@@ -25,8 +25,8 @@ CAST_SPLIT = 44
 
 
 def load_scale_rows(queue, plane, rows):
-    for q in range(4):
-        queue.dma_start(out=plane[32 * q : 32 * q + 4, :].bitcast(I32), in_=rows[0, 4 * q : 4 * q + 4, :].bitcast(I32))
+    for r in range(4):
+        queue.dma_start(out=plane[r:P:32, :].bitcast(I32), in_=rows[0, r:16:4, :].bitcast(I32))
 
 
 def tile_picked_yfism_sig_p_kernel(
@@ -35,21 +35,20 @@ def tile_picked_yfism_sig_p_kernel(
     nc = tc.nc
     with ExitStack() as ctx:
         keep = ctx.enter_context(tc.tile_pool(name="keep", bufs=1))
+        stage = ctx.enter_context(tc.tile_pool(name="stage", bufs=1))
         ring = ctx.enter_context(tc.tile_pool(name="ring", bufs=5))
-        psum_y = ctx.enter_context(tc.psum_pool(name="psum_y", bufs=3))
-        psum_s = ctx.enter_context(tc.psum_pool(name="psum_s", bufs=2))
-        psum_o = ctx.enter_context(tc.psum_pool(name="psum_o", bufs=3))
+        psum = ctx.enter_context(tc.psum_pool(name="psum", bufs=1))
 
         offs_sb = keep.tile([P, S // 16], U16, name="offs_sb")
         items_sb = keep.tile([P, R // 16], U16, name="items_sb")
         x_table = keep.tile([P, T], U32, name="x_table", align_bytes=64)
         x_table_scales = keep.tile([P, T], U8, name="x_table_scales", align_bytes=64)
         v_table = keep.tile([P, G], U32, name="v_table", align_bytes=64)
-        v_table_scales = keep.tile([P, G], U8, name="v_table_scales", tag="scales_then_others", align_bytes=64)
+        v_table_scales = keep.tile([P, G], U8, name="v_table_scales", align_bytes=64)
         bias_table = keep.tile([P, G], F32, name="bias_table", align_bytes=64)
         norm_sb = keep.tile([P, S], F32, name="norm_sb", align_bytes=64)
         half = H // 2
-        w_raw = [keep.tile([P, PACK, half], F32, name="w_raw%d" % a, align_bytes=64) for a in range(2)]
+        w_raw = [stage.tile([P, PACK, half], F32, name="w_raw%d" % a, align_bytes=64, offset=4096 * a) for a in range(2)]
         ident = keep.tile([P, P], F32, name="ident", align_bytes=64)
         warm_in = keep.tile([P, 1], F32, name="warm_in")
         warm_out = keep.tile([P, 1], F32, name="warm_out")
@@ -58,29 +57,28 @@ def tile_picked_yfism_sig_p_kernel(
         nc.gpsimd.memset(warm_in[:], 0.0)
         nc.scalar.activation(warm_out[:], warm_in[:], ACT.Sigmoid)
         nc.gpsimd.memset(v_table_scales[:].bitcast(I32), 0)
-        nc.vector.memset(bias_table[:], 0.0)
+        nc.vector.memset(bias_table[:].bitcast(I32), 0)
+        make_identity(nc, ident[:])
 
         w_rows = w1.rearrange("(p r) c -> p r c", r=PACK)
         nc.sync.dma_start(offs_sb[:], offs)
-        nc.sync.dma_start(out=x_table[:].bitcast(I32), in_=x_words[0].rearrange("p n r -> p (n r)").bitcast(I32))
+        nc.sync.dma_start(out=w_raw[0][:], in_=w_rows[:, :, :half])
         load_scale_rows(nc.sync, x_table_scales, x_scales)
-        for a in range(2):
-            nc.sync.dma_start(out=w_raw[a][:], in_=w_rows[:, :, a * half : (a + 1) * half])
+        nc.sync.dma_start(out=w_raw[1][:], in_=w_rows[:, :, half:])
+        nc.sync.dma_start(out=x_table[:].bitcast(I32), in_=x_words[0].rearrange("p n r -> p (n r)").bitcast(I32))
         nc.sync.dma_start(items_sb[:], items)
         nc.sync.dma_start(out=bias_table[0:1, :], in_=bias[0:1, :])
         nc.sync.dma_start(out=v_table[:].bitcast(I32), in_=v_words[0].rearrange("p n r -> p (n r)").bitcast(I32))
-        nc.sync.dma_start(out=norm_sb[:], in_=norm)
         load_scale_rows(nc.sync, v_table_scales, v_scales)
-        make_identity(nc, ident[:])
+        nc.sync.dma_start(out=norm_sb[:], in_=norm)
 
-        x_codes = keep.tile([P, S], U32, name="x_codes", align_bytes=64)
         x_plane = keep.tile([P, S], U8, name="x_plane", align_bytes=64)
-        nc.vector.tensor_copy(x_codes[:], x_table[:].indirect(offs_sb[:]))
         nc.vector.tensor_copy(x_plane[:], x_table_scales[:].indirect(offs_sb[:]))
 
-
-        w_grouped = keep.tile([P, PACK, P, PACK], BF16, name="w_grouped", align_bytes=64)
         rows = P // 2
+        w_grouped = stage.tile([P, PACK, P, PACK], BF16, name="w_grouped", align_bytes=64, offset=8192)
+        w_codes = keep.tile([P, PACK, P], U32, name="w_codes", align_bytes=64)
+        w_plane = keep.tile([P, PACK, P], U8, name="w_plane", tag="x_table_scales", align_bytes=64)
         for copy, a, lo, hi in (
             (nc.scalar.copy, 0, 0, rows),
             (nc.vector.tensor_copy, 1, 0, CAST_SPLIT),
@@ -90,30 +88,29 @@ def tile_picked_yfism_sig_p_kernel(
                 w_grouped[:, :, a * rows + lo : a * rows + hi, :].rearrange("p j m r -> p m j r"),
                 w_raw[a][:].rearrange("p r (m j) -> p m j r", j=PACK)[:, lo:hi],
             )
-        w_codes = keep.tile([P, PACK, P], U32, name="w_codes", align_bytes=64)
-        w_plane = keep.tile([P, PACK, P], U8, name="w_plane", align_bytes=64)
-        for j in range(PACK):
-            nc.vector.quantize_mx(
-                out=w_codes[:, j, :].bitcast(FP8X4),
-                scales=w_plane[:, j, :],
-                in_=w_grouped[:, j, :, :].rearrange("p m r -> p (m r)"),
-            )
-
-        v_codes = keep.tile([P, R], U32, name="v_codes", align_bytes=64)
-        v_plane = keep.tile([P, R], U8, name="v_plane", align_bytes=64)
+        nc.vector.quantize_mx(
+            out=w_codes[:].rearrange("p j m -> p (j m)").bitcast(FP8X4),
+            scales=w_plane[:].rearrange("p j m -> p (j m)"),
+            in_=w_grouped[:].rearrange("p j m r -> p (j m r)"),
+        )
+        x_codes = []
+        for first, tiles in ((0, 1), (1, 1), (2, 2)):
+            picked = stage.tile([P, tiles * P], U32, name="x_codes%d" % first, align_bytes=64, offset=4096 + 512 * first)
+            nc.vector.tensor_copy(picked[:], x_table[:].indirect(offs_sb[:, 8 * first : 8 * (first + tiles)]))
+            x_codes.extend(picked[:, a * P : (a + 1) * P] for a in range(tiles))
 
         sums, z_bf, z_mx, y_banks = {}, {}, {}, {}
         y_sb = [keep.tile([P, D, 2, BASKETS, PACK], F32, name="y_sb%d" % s, align_bytes=64) for s in range(2)]
 
         def project(a):
             cols = slice(a * P, (a + 1) * P)
-            y_banks[a] = psum_y.tile([P, PACK, P], F32, name="y")
+            y_banks[a] = psum.tile([P, PACK, P], F32, name="y", tag="bank%d" % (0, 1, 2, 1)[a])
             for j in range(PACK):
                 nc.tensor.matmul_mx(
                     out=y_banks[a][:, j, :],
                     lhsT=w_codes[:, j, :].bitcast(FP8X4),
                     lhsT_scale=w_plane[:, j, :],
-                    rhs=x_codes[:, cols].bitcast(FP8X4),
+                    rhs=x_codes[a].bitcast(FP8X4),
                     rhs_scale=x_plane[:, cols],
                     start=True,
                     stop=True,
@@ -122,7 +119,7 @@ def tile_picked_yfism_sig_p_kernel(
             nc.scalar.copy(y_sb[pair][:, :, side], y_banks[a][:].rearrange("p j (v d) -> p d v j", d=D))
 
         def basket_sums(pair):
-            turned = psum_o.tile([P, P], F32, name="turned")
+            turned = psum.tile([P, P], F32, name="turned", tag="bank7")
             for d in range(D):
                 nc.tensor.matmul(
                     turned[:],
@@ -134,7 +131,7 @@ def tile_picked_yfism_sig_p_kernel(
                 )
             turned_sb = ring.tile([P, P], F32, name="turned_sb", align_bytes=64)
             nc.scalar.copy(turned_sb[:], turned[:])
-            sums[pair] = psum_s.tile([P, 2, BASKETS, PACK], F32, name="sums")
+            sums[pair] = psum.tile([P, 2, BASKETS, PACK], F32, name="sums", tag="bank%d" % (5 + pair))
             nc.tensor.transpose(sums[pair][:].rearrange("p s v j -> p (s v j)"), turned_sb[:], ident[:])
 
         def leave_out(a):
@@ -163,14 +160,45 @@ def tile_picked_yfism_sig_p_kernel(
             )
             z_mx[a] = (z_codes, z_plane)
 
-        def score_direct(a, parts, pool, tag):
+        def score(a, copy_out, banks):
             z_codes, z_plane = z_mx[a]
-            width = R // parts
-            sc = pool.tile([P, R], F32, name=tag)
-            for c in range(parts):
+            blocks = TILES // len(banks)
+            width = blocks * P
+            probs = []
+            for c, (score_bank, turn_bank) in enumerate(banks):
+                sc = psum.tile([P, blocks, P], F32, name="sc", tag=score_bank)
+                for b in range(blocks):
+                    cols = slice(c * width + b * P, c * width + (b + 1) * P)
+                    nc.tensor.matmul_mx(
+                        out=sc[:, b, :],
+                        lhsT=v_codes[:, cols].bitcast(FP8X4),
+                        lhsT_scale=v_plane[:, cols],
+                        rhs=z_codes[:].bitcast(FP8X4),
+                        rhs_scale=z_plane[:],
+                        start=True,
+                        stop=True,
+                    )
+                part = ring.tile([P, blocks, P], F32, name="probs", align_bytes=64)
+                for b in range(blocks):
+                    g = c * blocks + b
+                    nc.scalar.activation(part[:, b, :], sc[:, b, :], ACT.Sigmoid, bias=bias_cols[:, g : g + 1])
+                probs.append(part)
+            for c, (score_bank, turn_bank) in enumerate(banks):
+                turned = psum.tile([P, blocks, P], F32, name="probs_turned", tag=turn_bank)
+                for b in range(blocks):
+                    nc.tensor.transpose(turned[:, b, :], probs[c][:, b, :], ident[:])
+                result = ring.tile([P, width], F32, name="result", align_bytes=64)
+                copy_out(result[:], turned[:].rearrange("p b g -> p (b g)"))
+                nc.sync.dma_start(out=out[a * P : (a + 1) * P, c * width : (c + 1) * width], in_=result[:])
+
+        def score_direct(a, banks):
+            z_codes, z_plane = z_mx[a]
+            width = R // len(banks)
+            for c, bank in enumerate(banks):
                 cols = slice(c * width, (c + 1) * width)
+                sc = psum.tile([P, width], F32, name="sc_direct", tag=bank)
                 nc.tensor.matmul_mx(
-                    out=sc[:, cols],
+                    out=sc[:],
                     lhsT=z_codes[:].bitcast(FP8X4),
                     lhsT_scale=z_plane[:],
                     rhs=v_codes[:, cols].bitcast(FP8X4),
@@ -178,37 +206,11 @@ def tile_picked_yfism_sig_p_kernel(
                     start=True,
                     stop=True,
                 )
-            for c in range(parts):
-                cols = slice(c * width, (c + 1) * width)
                 logits = ring.tile([P, width], F32, name="logits", align_bytes=64)
-                nc.vector.tensor_tensor(logits[:], sc[:, cols], bias_rows[:, cols], ALU.add)
+                nc.vector.tensor_tensor(logits[:], sc[:], bias_rows[:, cols], ALU.add)
                 result = ring.tile([P, width], F32, name="result", align_bytes=64)
                 nc.scalar.activation(result[:], logits[:], ACT.Sigmoid)
                 nc.sync.dma_start(out=out[a * P : (a + 1) * P, cols], in_=result[:])
-
-        def score_turned(a):
-            z_codes, z_plane = z_mx[a]
-            sc = psum_y.tile([P, TILES, P], F32, name="y")
-            for b in range(TILES):
-                cols = slice(b * P, (b + 1) * P)
-                nc.tensor.matmul_mx(
-                    out=sc[:, b, :],
-                    lhsT=v_codes[:, cols].bitcast(FP8X4),
-                    lhsT_scale=v_plane[:, cols],
-                    rhs=z_codes[:].bitcast(FP8X4),
-                    rhs_scale=z_plane[:],
-                    start=True,
-                    stop=True,
-                )
-            probs = ring.tile([P, TILES, P], F32, name="probs", align_bytes=64)
-            for b in range(TILES):
-                nc.scalar.activation(probs[:, b, :], sc[:, b, :], ACT.Sigmoid, bias=bias_cols[:, b : b + 1])
-            turned = psum_o.tile([P, TILES, P], F32, name="turned")
-            for b in range(TILES):
-                nc.tensor.transpose(turned[:, b, :], probs[:, b, :], ident[:])
-            result = ring.tile([P, R], F32, name="result", align_bytes=64)
-            nc.scalar.copy(result[:], turned[:].rearrange("p b g -> p (b g)"))
-            nc.sync.dma_start(out=out[a * P : (a + 1) * P, :], in_=result[:])
 
         project(0)
         project(1)
@@ -216,35 +218,38 @@ def tile_picked_yfism_sig_p_kernel(
         project(2)
         project(3)
         basket_sums(1)
-        bias_picked = keep.tile([P, R], F32, name="bias_picked", align_bytes=64)
+        bias_picked = stage.tile([P, R], F32, name="bias_picked", align_bytes=64, offset=8192)
         nc.vector.tensor_copy(bias_picked[:], bias_table[:].indirect(items_sb[:]))
-        bias_turned = psum_o.tile([P, TILES, P], F32, name="turned")
+        v_codes = keep.tile([P, R], U32, name="v_codes", tag="x_table", align_bytes=64)
+        nc.vector.tensor_copy(v_codes[:], v_table[:].indirect(items_sb[:]))
+        v_plane = keep.tile([P, R], U8, name="v_plane", tag="bias_table", align_bytes=64)
+        nc.vector.tensor_copy(v_plane[:], v_table_scales[:].indirect(items_sb[:]))
+        others = keep.tile([P, TILES, BASKETS, D, PACK], F32, name="others", tag="v_table_scales", align_bytes=64)
+
+        bias_turned = psum.tile([P, TILES, P], F32, name="bias_turned", tag="bank1")
         for b in range(TILES):
             nc.tensor.transpose(bias_turned[:, b, :], bias_picked[:, b * P : (b + 1) * P], ident[:])
         bias_cols = keep.tile([P, TILES], F32, name="bias_cols")
         nc.scalar.copy(bias_cols[:], bias_turned[:, :, 0])
-        bias_spread = psum_o.tile([P, TILES, P], F32, name="turned")
+        bias_spread = psum.tile([P, TILES, P], F32, name="bias_spread", tag="bank2")
         for b in range(TILES):
             nc.tensor.transpose(bias_spread[:, b, :], bias_cols[:, b : b + 1].to_broadcast([P, P]), ident[:])
         bias_rows = keep.tile([P, R], F32, name="bias_rows", align_bytes=64)
         nc.scalar.copy(bias_rows[:], bias_spread[:].rearrange("p b g -> p (b g)"))
 
-        nc.vector.tensor_copy(v_codes[:], v_table[:].indirect(items_sb[:]))
-        nc.vector.tensor_copy(v_plane[:], v_table_scales[:].indirect(items_sb[:]))
-        others = keep.tile([P, TILES, BASKETS, D, PACK], F32, name="others", tag="scales_then_others", align_bytes=64)
         leave_out(0)
         leave_out(1)
         scale_by_norm(0)
-        leave_out(2)
         quantize_z(0)
-        score_turned(0)
+        score(0, nc.scalar.copy, [("bank0", "bank4")])
         scale_by_norm(1)
-        scale_by_norm(2)
+        leave_out(2)
         quantize_z(1)
-        score_turned(1)
+        score(1, nc.scalar.copy, [("bank1", "bank7")])
+        scale_by_norm(2)
         leave_out(3)
         quantize_z(2)
         scale_by_norm(3)
+        score_direct(2, ["bank3"])
         quantize_z(3)
-        score_direct(2, 1, psum_s, "sums")
-        score_direct(3, 2, psum_s, "sums")
+        score_direct(3, ["bank5", "bank6"])

@@ -36,7 +36,7 @@ def tile_picked_yfism_sig_p_kernel(
     with ExitStack() as ctx:
         keep = ctx.enter_context(tc.tile_pool(name="keep", bufs=1))
         stage = ctx.enter_context(tc.tile_pool(name="stage", bufs=1))
-        ring = ctx.enter_context(tc.tile_pool(name="ring", bufs=5))
+        ring = ctx.enter_context(tc.tile_pool(name="ring", bufs=6))
         psum = ctx.enter_context(tc.psum_pool(name="psum", bufs=1))
 
         offs_sb = keep.tile([P, S // 16], U16, name="offs_sb")
@@ -104,7 +104,7 @@ def tile_picked_yfism_sig_p_kernel(
 
         def project(a):
             cols = slice(a * P, (a + 1) * P)
-            y_banks[a] = psum.tile([P, PACK, P], F32, name="y", tag="bank%d" % (0, 1, 2, 1)[a])
+            y_banks[a] = psum.tile([P, PACK, P], F32, name="y", tag="bank%d" % a)
             for j in range(PACK):
                 nc.tensor.matmul_mx(
                     out=y_banks[a][:, j, :],
@@ -119,7 +119,7 @@ def tile_picked_yfism_sig_p_kernel(
             nc.scalar.copy(y_sb[pair][:, :, side], y_banks[a][:].rearrange("p j (v d) -> p d v j", d=D))
 
         def basket_sums(pair):
-            turned = psum.tile([P, P], F32, name="turned", tag="bank7")
+            turned = psum.tile([P, P], F32, name="turned", tag="bank%d" % (7, 4)[pair])
             for d in range(D):
                 nc.tensor.matmul(
                     turned[:],
@@ -191,11 +191,10 @@ def tile_picked_yfism_sig_p_kernel(
                 copy_out(result[:], turned[:].rearrange("p b g -> p (b g)"))
                 nc.sync.dma_start(out=out[a * P : (a + 1) * P, c * width : (c + 1) * width], in_=result[:])
 
-        def score_direct(a, banks):
+        def score_direct(a, parts):
             z_codes, z_plane = z_mx[a]
-            width = R // len(banks)
-            for c, bank in enumerate(banks):
-                cols = slice(c * width, (c + 1) * width)
+            for first, width, bank, queue in parts:
+                cols = slice(first, first + width)
                 sc = psum.tile([P, width], F32, name="sc_direct", tag=bank)
                 nc.tensor.matmul_mx(
                     out=sc[:],
@@ -210,7 +209,7 @@ def tile_picked_yfism_sig_p_kernel(
                 nc.vector.tensor_tensor(logits[:], sc[:], bias_rows[:, cols], ALU.add)
                 result = ring.tile([P, width], F32, name="result", align_bytes=64)
                 nc.scalar.activation(result[:], logits[:], ACT.Sigmoid)
-                nc.sync.dma_start(out=out[a * P : (a + 1) * P, cols], in_=result[:])
+                queue.dma_start(out=out[a * P : (a + 1) * P, cols], in_=result[:])
 
         project(0)
         project(1)
@@ -226,7 +225,7 @@ def tile_picked_yfism_sig_p_kernel(
         nc.vector.tensor_copy(v_plane[:], v_table_scales[:].indirect(items_sb[:]))
         others = keep.tile([P, TILES, BASKETS, D, PACK], F32, name="others", tag="v_table_scales", align_bytes=64)
 
-        bias_turned = psum.tile([P, TILES, P], F32, name="bias_turned", tag="bank1")
+        bias_turned = psum.tile([P, TILES, P], F32, name="bias_turned", tag="bank7")
         for b in range(TILES):
             nc.tensor.transpose(bias_turned[:, b, :], bias_picked[:, b * P : (b + 1) * P], ident[:])
         bias_cols = keep.tile([P, TILES], F32, name="bias_cols")
@@ -241,15 +240,16 @@ def tile_picked_yfism_sig_p_kernel(
         leave_out(1)
         scale_by_norm(0)
         quantize_z(0)
-        score(0, nc.scalar.copy, [("bank0", "bank4")])
+        score(0, nc.scalar.copy, [("bank0", "bank3")])
         scale_by_norm(1)
         leave_out(2)
         quantize_z(1)
-        score(1, nc.scalar.copy, [("bank1", "bank7")])
+        score(1, nc.scalar.copy, [("bank1", "bank4")])
         scale_by_norm(2)
         leave_out(3)
         quantize_z(2)
         scale_by_norm(3)
-        score_direct(2, ["bank3"])
+        score_direct(2, [(0, 256, "bank7", nc.sync)])
         quantize_z(3)
-        score_direct(3, ["bank5", "bank6"])
+        score_direct(2, [(256, 256, "bank2", nc.sync)])
+        score_direct(3, [(0, 256, "bank5", nc.sync), (256, 256, "bank6", nc.scalar)])

@@ -15,18 +15,38 @@ U8 = mybir.dt.uint8
 FP8X4 = mybir.dt.float8_e4m3fn_x4
 ALU = mybir.AluOpType
 ACT = mybir.ActivationFunctionType
-AX = mybir.AxisListType
 
 P = 128
 PACK = 4
 TILES = S // P
 BASKETS = P // D
+LIST_COLS = P // 16
+HALF = 256
+GROUPS = HALF // PACK
 CAST_SPLIT = 44
+RING = 6
+W_BYTES = PACK * HALF * 4
 
 
-def load_scale_rows(queue, plane, rows):
+def load_scale_rows(nc, plane, rows):
     for r in range(4):
-        queue.dma_start(out=plane[r:P:32, :].bitcast(I32), in_=rows[0, r:16:4, :].bitcast(I32))
+        nc.sync.dma_start(out=plane[r:P:32, :].bitcast(I32), in_=rows[0, r:16:4, :].bitcast(I32))
+
+
+def load_words(nc, table, words):
+    nc.sync.dma_start(out=table[:].bitcast(I32), in_=words[0].rearrange("p n r -> p (n r)").bitcast(I32))
+
+
+def product(nc, acc, stationary, moving):
+    nc.tensor.matmul_mx(
+        out=acc,
+        lhsT=stationary[0].bitcast(FP8X4),
+        lhsT_scale=stationary[1],
+        rhs=moving[0].bitcast(FP8X4),
+        rhs_scale=moving[1],
+        start=True,
+        stop=True,
+    )
 
 
 def tile_picked_yfism_sig_p_kernel(
@@ -36,7 +56,7 @@ def tile_picked_yfism_sig_p_kernel(
     with ExitStack() as ctx:
         keep = ctx.enter_context(tc.tile_pool(name="keep", bufs=1))
         stage = ctx.enter_context(tc.tile_pool(name="stage", bufs=1))
-        ring = ctx.enter_context(tc.tile_pool(name="ring", bufs=6))
+        ring = ctx.enter_context(tc.tile_pool(name="ring", bufs=RING))
         psum = ctx.enter_context(tc.psum_pool(name="psum", bufs=1))
 
         offs_sb = keep.tile([P, S // 16], U16, name="offs_sb")
@@ -47,8 +67,9 @@ def tile_picked_yfism_sig_p_kernel(
         v_table_scales = keep.tile([P, G], U8, name="v_table_scales", align_bytes=64)
         bias_table = keep.tile([P, G], F32, name="bias_table", align_bytes=64)
         norm_sb = keep.tile([P, S], F32, name="norm_sb", align_bytes=64)
-        half = H // 2
-        w_raw = [stage.tile([P, PACK, half], F32, name="w_raw%d" % a, align_bytes=64, offset=4096 * a) for a in range(2)]
+        w_raw = [
+            stage.tile([P, PACK, HALF], F32, name="w_raw%d" % h, align_bytes=64, offset=W_BYTES * h) for h in range(2)
+        ]
         ident = keep.tile([P, P], F32, name="ident", align_bytes=64)
         warm_in = keep.tile([P, 1], F32, name="warm_in")
         warm_out = keep.tile([P, 1], F32, name="warm_out")
@@ -61,65 +82,59 @@ def tile_picked_yfism_sig_p_kernel(
         make_identity(nc, ident[:])
 
         w_rows = w1.rearrange("(p r) c -> p r c", r=PACK)
+        nc.sync.dma_start(out=w_raw[0][:], in_=w_rows[:, :, :HALF])
         nc.sync.dma_start(offs_sb[:], offs)
-        nc.sync.dma_start(out=w_raw[0][:], in_=w_rows[:, :, :half])
-        load_scale_rows(nc.sync, x_table_scales, x_scales)
-        nc.sync.dma_start(out=w_raw[1][:], in_=w_rows[:, :, half:])
-        nc.sync.dma_start(out=x_table[:].bitcast(I32), in_=x_words[0].rearrange("p n r -> p (n r)").bitcast(I32))
+        load_scale_rows(nc, x_table_scales, x_scales)
+        nc.sync.dma_start(out=w_raw[1][:], in_=w_rows[:, :, HALF:])
+        load_words(nc, x_table, x_words)
         nc.sync.dma_start(items_sb[:], items)
         nc.sync.dma_start(out=bias_table[0:1, :], in_=bias[0:1, :])
-        nc.sync.dma_start(out=v_table[:].bitcast(I32), in_=v_words[0].rearrange("p n r -> p (n r)").bitcast(I32))
-        load_scale_rows(nc.sync, v_table_scales, v_scales)
+        load_words(nc, v_table, v_words)
+        load_scale_rows(nc, v_table_scales, v_scales)
         nc.sync.dma_start(out=norm_sb[:], in_=norm)
 
         x_plane = keep.tile([P, S], U8, name="x_plane", align_bytes=64)
         nc.vector.tensor_copy(x_plane[:], x_table_scales[:].indirect(offs_sb[:]))
 
-        rows = P // 2
-        w_grouped = stage.tile([P, PACK, P, PACK], BF16, name="w_grouped", align_bytes=64, offset=8192)
+        w_grouped = stage.tile([P, PACK, P, PACK], BF16, name="w_grouped", align_bytes=64, offset=2 * W_BYTES)
         w_codes = keep.tile([P, PACK, P], U32, name="w_codes", align_bytes=64)
         w_plane = keep.tile([P, PACK, P], U8, name="w_plane", tag="x_table_scales", align_bytes=64)
-        for copy, a, lo, hi in (
-            (nc.scalar.copy, 0, 0, rows),
+        for cast, h, lo, hi in (
+            (nc.scalar.copy, 0, 0, GROUPS),
             (nc.vector.tensor_copy, 1, 0, CAST_SPLIT),
-            (nc.scalar.copy, 1, CAST_SPLIT, rows),
+            (nc.scalar.copy, 1, CAST_SPLIT, GROUPS),
         ):
-            copy(
-                w_grouped[:, :, a * rows + lo : a * rows + hi, :].rearrange("p j m r -> p m j r"),
-                w_raw[a][:].rearrange("p r (m j) -> p m j r", j=PACK)[:, lo:hi],
+            cast(
+                w_grouped[:, :, h * GROUPS + lo : h * GROUPS + hi, :].rearrange("p j m r -> p m j r"),
+                w_raw[h][:].rearrange("p r (m j) -> p m j r", j=PACK)[:, lo:hi],
             )
         nc.vector.quantize_mx(
             out=w_codes[:].rearrange("p j m -> p (j m)").bitcast(FP8X4),
             scales=w_plane[:].rearrange("p j m -> p (j m)"),
             in_=w_grouped[:].rearrange("p j m r -> p (j m r)"),
         )
-        x_codes = []
-        for first, tiles in ((0, 1), (1, 1), (2, 2)):
-            picked = stage.tile([P, tiles * P], U32, name="x_codes%d" % first, align_bytes=64, offset=4096 + 512 * first)
-            nc.vector.tensor_copy(picked[:], x_table[:].indirect(offs_sb[:, 8 * first : 8 * (first + tiles)]))
-            x_codes.extend(picked[:, a * P : (a + 1) * P] for a in range(tiles))
 
-        sums, z_bf, z_mx, y_banks = {}, {}, {}, {}
-        y_sb = [keep.tile([P, D, 2, BASKETS, PACK], F32, name="y_sb%d" % s, align_bytes=64) for s in range(2)]
+        x_codes = []
+        for first, count in ((0, 1), (1, 1), (2, 2)):
+            picked = stage.tile(
+                [P, count * P], U32, name="x_codes%d" % first, align_bytes=64, offset=W_BYTES + 4 * P * first
+            )
+            entries = offs_sb[:, LIST_COLS * first : LIST_COLS * (first + count)]
+            nc.vector.tensor_copy(picked[:], x_table[:].indirect(entries))
+            x_codes.extend(picked[:, n * P : (n + 1) * P] for n in range(count))
+
+        sums, z_bf, z_mx = {}, {}, {}
+        y_sb = [keep.tile([P, D, 2, BASKETS, PACK], F32, name="y_sb%d" % pair, align_bytes=64) for pair in range(2)]
 
         def project(a):
-            cols = slice(a * P, (a + 1) * P)
-            y_banks[a] = psum.tile([P, PACK, P], F32, name="y", tag="bank%d" % a)
+            y = psum.tile([P, PACK, P], F32, name="y", tag="bank%d" % a)
             for j in range(PACK):
-                nc.tensor.matmul_mx(
-                    out=y_banks[a][:, j, :],
-                    lhsT=w_codes[:, j, :].bitcast(FP8X4),
-                    lhsT_scale=w_plane[:, j, :],
-                    rhs=x_codes[a].bitcast(FP8X4),
-                    rhs_scale=x_plane[:, cols],
-                    start=True,
-                    stop=True,
-                )
+                product(nc, y[:, j, :], (w_codes[:, j, :], w_plane[:, j, :]), (x_codes[a], x_plane[:, a * P : (a + 1) * P]))
             pair, side = divmod(a, 2)
-            nc.scalar.copy(y_sb[pair][:, :, side], y_banks[a][:].rearrange("p j (v d) -> p d v j", d=D))
+            nc.scalar.copy(y_sb[pair][:, :, side], y[:].rearrange("p j (v d) -> p d v j", d=D))
 
-        def basket_sums(pair):
-            turned = psum.tile([P, P], F32, name="turned", tag="bank%d" % (7, 4)[pair])
+        def basket_sums(pair, adding_bank, sums_bank):
+            turned = psum.tile([P, P], F32, name="turned", tag=adding_bank)
             for d in range(D):
                 nc.tensor.matmul(
                     turned[:],
@@ -131,7 +146,7 @@ def tile_picked_yfism_sig_p_kernel(
                 )
             turned_sb = ring.tile([P, P], F32, name="turned_sb", align_bytes=64)
             nc.scalar.copy(turned_sb[:], turned[:])
-            sums[pair] = psum.tile([P, 2, BASKETS, PACK], F32, name="sums", tag="bank%d" % (5 + pair))
+            sums[pair] = psum.tile([P, 2, BASKETS, PACK], F32, name="sums", tag=sums_bank)
             nc.tensor.transpose(sums[pair][:].rearrange("p s v j -> p (s v j)"), turned_sb[:], ident[:])
 
         def leave_out(a):
@@ -158,66 +173,41 @@ def tile_picked_yfism_sig_p_kernel(
             nc.vector.quantize_mx(
                 out=z_codes[:].bitcast(FP8X4), scales=z_plane[:], in_=z_bf[a][:].rearrange("p t j -> p (t j)")
             )
-            z_mx[a] = (z_codes, z_plane)
+            z_mx[a] = (z_codes[:], z_plane[:])
 
-        def score(a, copy_out, banks):
-            z_codes, z_plane = z_mx[a]
-            blocks = TILES // len(banks)
-            width = blocks * P
-            probs = []
-            for c, (score_bank, turn_bank) in enumerate(banks):
-                sc = psum.tile([P, blocks, P], F32, name="sc", tag=score_bank)
-                for b in range(blocks):
-                    cols = slice(c * width + b * P, c * width + (b + 1) * P)
-                    nc.tensor.matmul_mx(
-                        out=sc[:, b, :],
-                        lhsT=v_codes[:, cols].bitcast(FP8X4),
-                        lhsT_scale=v_plane[:, cols],
-                        rhs=z_codes[:].bitcast(FP8X4),
-                        rhs_scale=z_plane[:],
-                        start=True,
-                        stop=True,
-                    )
-                part = ring.tile([P, blocks, P], F32, name="probs", align_bytes=64)
-                for b in range(blocks):
-                    g = c * blocks + b
-                    nc.scalar.activation(part[:, b, :], sc[:, b, :], ACT.Sigmoid, bias=bias_cols[:, g : g + 1])
-                probs.append(part)
-            for c, (score_bank, turn_bank) in enumerate(banks):
-                turned = psum.tile([P, blocks, P], F32, name="probs_turned", tag=turn_bank)
-                for b in range(blocks):
-                    nc.tensor.transpose(turned[:, b, :], probs[c][:, b, :], ident[:])
-                result = ring.tile([P, width], F32, name="result", align_bytes=64)
-                copy_out(result[:], turned[:].rearrange("p b g -> p (b g)"))
-                nc.sync.dma_start(out=out[a * P : (a + 1) * P, c * width : (c + 1) * width], in_=result[:])
+        def score_turned(a, score_bank, turn_bank):
+            scores = psum.tile([P, TILES, P], F32, name="scores_turned", tag=score_bank)
+            for b in range(TILES):
+                targets = slice(b * P, (b + 1) * P)
+                product(nc, scores[:, b, :], (v_codes[:, targets], v_plane[:, targets]), z_mx[a])
+            probs = ring.tile([P, TILES, P], F32, name="probs", align_bytes=64)
+            for b in range(TILES):
+                nc.scalar.activation(probs[:, b, :], scores[:, b, :], ACT.Sigmoid, bias=bias_cols[:, b : b + 1])
+            probs_back = psum.tile([P, TILES, P], F32, name="probs_back", tag=turn_bank)
+            for b in range(TILES):
+                nc.tensor.transpose(probs_back[:, b, :], probs[:, b, :], ident[:])
+            result = ring.tile([P, R], F32, name="result", align_bytes=64)
+            nc.scalar.copy(result[:], probs_back[:].rearrange("p b g -> p (b g)"))
+            nc.sync.dma_start(out=out[a * P : (a + 1) * P, :], in_=result[:])
 
-        def score_direct(a, parts):
-            z_codes, z_plane = z_mx[a]
-            for first, width, bank, queue in parts:
-                cols = slice(first, first + width)
-                sc = psum.tile([P, width], F32, name="sc_direct", tag=bank)
-                nc.tensor.matmul_mx(
-                    out=sc[:],
-                    lhsT=z_codes[:].bitcast(FP8X4),
-                    lhsT_scale=z_plane[:],
-                    rhs=v_codes[:, cols].bitcast(FP8X4),
-                    rhs_scale=v_plane[:, cols],
-                    start=True,
-                    stop=True,
-                )
-                logits = ring.tile([P, width], F32, name="logits", align_bytes=64)
-                nc.vector.tensor_tensor(logits[:], sc[:], bias_rows[:, cols], ALU.add)
-                result = ring.tile([P, width], F32, name="result", align_bytes=64)
-                nc.scalar.activation(result[:], logits[:], ACT.Sigmoid)
-                queue.dma_start(out=out[a * P : (a + 1) * P, cols], in_=result[:])
+        def score_direct(a, h, bank, queue):
+            targets = slice(h * HALF, (h + 1) * HALF)
+            scores = psum.tile([P, HALF], F32, name="scores_direct", tag=bank)
+            product(nc, scores[:], z_mx[a], (v_codes[:, targets], v_plane[:, targets]))
+            logits = ring.tile([P, HALF], F32, name="logits", align_bytes=64)
+            nc.vector.tensor_tensor(logits[:], scores[:], bias_rows[:, targets], ALU.add)
+            result = ring.tile([P, HALF], F32, name="result", align_bytes=64)
+            nc.scalar.activation(result[:], logits[:], ACT.Sigmoid)
+            queue.dma_start(out=out[a * P : (a + 1) * P, targets], in_=result[:])
 
         project(0)
         project(1)
-        basket_sums(0)
+        basket_sums(0, "bank7", "bank5")
         project(2)
         project(3)
-        basket_sums(1)
-        bias_picked = stage.tile([P, R], F32, name="bias_picked", align_bytes=64, offset=8192)
+        basket_sums(1, "bank4", "bank6")
+
+        bias_picked = stage.tile([P, R], F32, name="bias_picked", align_bytes=64, offset=2 * W_BYTES)
         nc.vector.tensor_copy(bias_picked[:], bias_table[:].indirect(items_sb[:]))
         v_codes = keep.tile([P, R], U32, name="v_codes", tag="x_table", align_bytes=64)
         nc.vector.tensor_copy(v_codes[:], v_table[:].indirect(items_sb[:]))
@@ -225,7 +215,7 @@ def tile_picked_yfism_sig_p_kernel(
         nc.vector.tensor_copy(v_plane[:], v_table_scales[:].indirect(items_sb[:]))
         others = keep.tile([P, TILES, BASKETS, D, PACK], F32, name="others", tag="v_table_scales", align_bytes=64)
 
-        bias_turned = psum.tile([P, TILES, P], F32, name="bias_turned", tag="bank7")
+        bias_turned = psum.tile([P, TILES, P], F32, name="bias_turned", tag="bank4")
         for b in range(TILES):
             nc.tensor.transpose(bias_turned[:, b, :], bias_picked[:, b * P : (b + 1) * P], ident[:])
         bias_cols = keep.tile([P, TILES], F32, name="bias_cols")
@@ -240,16 +230,17 @@ def tile_picked_yfism_sig_p_kernel(
         leave_out(1)
         scale_by_norm(0)
         quantize_z(0)
-        score(0, nc.scalar.copy, [("bank0", "bank3")])
+        score_turned(0, "bank0", "bank3")
         scale_by_norm(1)
         leave_out(2)
         quantize_z(1)
-        score(1, nc.scalar.copy, [("bank1", "bank4")])
+        score_turned(1, "bank1", "bank4")
         scale_by_norm(2)
         leave_out(3)
         quantize_z(2)
         scale_by_norm(3)
-        score_direct(2, [(0, 256, "bank7", nc.sync)])
+        score_direct(2, 0, "bank7", nc.sync)
         quantize_z(3)
-        score_direct(2, [(256, 256, "bank2", nc.sync)])
-        score_direct(3, [(0, 256, "bank5", nc.sync), (256, 256, "bank6", nc.scalar)])
+        score_direct(2, 1, "bank2", nc.sync)
+        score_direct(3, 0, "bank5", nc.sync)
+        score_direct(3, 1, "bank6", nc.scalar)

@@ -77,8 +77,8 @@ def tile_picked_yfism_sig_p_kernel(
         nc.gpsimd.memset(x_table_scales[:].bitcast(I32), 0)
         nc.gpsimd.memset(warm_in[:], 0.0)
         nc.scalar.activation(warm_out[:], warm_in[:], ACT.Sigmoid)
+        nc.gpsimd.memset(bias_table[:].bitcast(I32), 0)
         nc.gpsimd.memset(v_table_scales[:].bitcast(I32), 0)
-        nc.vector.memset(bias_table[:].bitcast(I32), 0)
         make_identity(nc, ident[:])
 
         w_rows = w1.rearrange("(p r) c -> p r c", r=PACK)
@@ -131,7 +131,9 @@ def tile_picked_yfism_sig_p_kernel(
             for j in range(PACK):
                 product(nc, y[:, j, :], (w_codes[:, j, :], w_plane[:, j, :]), (x_codes[a], x_plane[:, a * P : (a + 1) * P]))
             pair, side = divmod(a, 2)
-            nc.scalar.copy(y_sb[pair][:, :, side], y[:].rearrange("p j (v d) -> p d v j", d=D))
+            by_item = y[:].rearrange("p j (v d) -> p d v j", d=D)
+            for part in (slice(0, D // 2), slice(D // 2, D)) if side else (slice(0, D),):
+                nc.scalar.copy(y_sb[pair][:, part, side], by_item[:, part])
 
         def basket_sums(pair, adding_bank, sums_bank):
             turned = psum.tile([P, P], F32, name="turned", tag=adding_bank)

@@ -24,7 +24,8 @@ LIST_COLS = P // 16
 HALF = 256
 GROUPS = HALF // PACK
 CAST_SPLIT = 44
-RING = 6
+LAST_CUT = 6
+RING = 8
 W_BYTES = PACK * HALF * 4
 
 
@@ -123,7 +124,7 @@ def tile_picked_yfism_sig_p_kernel(
             nc.vector.tensor_copy(picked[:], x_table[:].indirect(entries))
             x_codes.extend(picked[:, n * P : (n + 1) * P] for n in range(count))
 
-        sums, z_bf, z_mx = {}, {}, {}
+        sums, z_bf, z_mx, others_ps = {}, {}, {}, []
         y_sb = [keep.tile([P, D, 2, BASKETS, PACK], F32, name="y_sb%d" % pair, align_bytes=64) for pair in range(2)]
 
         def project(a):
@@ -132,10 +133,11 @@ def tile_picked_yfism_sig_p_kernel(
                 product(nc, y[:, j, :], (w_codes[:, j, :], w_plane[:, j, :]), (x_codes[a], x_plane[:, a * P : (a + 1) * P]))
             pair, side = divmod(a, 2)
             by_item = y[:].rearrange("p j (v d) -> p d v j", d=D)
-            for part in (slice(0, D // 2), slice(D // 2, D)) if side else (slice(0, D),):
+            cut = (D, D // 2, D, LAST_CUT)[a]
+            for part in (slice(0, cut), slice(cut, D)) if side else (slice(0, D),):
                 nc.scalar.copy(y_sb[pair][:, part, side], by_item[:, part])
 
-        def basket_sums(pair, adding_bank, sums_bank):
+        def add_items(pair, adding_bank):
             turned = psum.tile([P, P], F32, name="turned", tag=adding_bank)
             for d in range(D):
                 nc.tensor.matmul(
@@ -148,15 +150,58 @@ def tile_picked_yfism_sig_p_kernel(
                 )
             turned_sb = ring.tile([P, P], F32, name="turned_sb", align_bytes=64)
             nc.scalar.copy(turned_sb[:], turned[:])
+            return turned_sb
+
+        def basket_sums(pair, adding_bank, sums_bank):
+            turned_sb = add_items(pair, adding_bank)
             sums[pair] = psum.tile([P, 2, BASKETS, PACK], F32, name="sums", tag=sums_bank)
             nc.tensor.transpose(sums[pair][:].rearrange("p s v j -> p (s v j)"), turned_sb[:], ident[:])
 
-        def leave_out(a):
-            pair, side = divmod(a, 2)
+        def turn_items(pair, item_banks, adding_bank):
+            total = add_items(pair, adding_bank)
+            minus_y = keep.tile([P, D, P], F32, name="minus_y", align_bytes=64)
+            for h, bank in enumerate(item_banks):
+                items_turned = psum.tile([P, D // 2, P], F32, name="items_turned", tag=bank)
+                for n in range(D // 2):
+                    item = y_sb[pair][:, h * D // 2 + n].rearrange("p s v j -> p (s v j)")
+                    nc.tensor.transpose(items_turned[:, n, :], item, ident[:])
+                nc.scalar.activation(minus_y[:, h * D // 2 : (h + 1) * D // 2], items_turned[:], ACT.Copy, scale=-1.0)
+            return total, minus_y
+
+        def turn_back(total, minus_y, others_banks):
+            for h, bank in enumerate(others_banks):
+                half = psum.tile([P, D // 2, 2, BASKETS, PACK], F32, name="others_ps", tag=bank)
+                terms = [total[:]] * (D // 2) + [minus_y[:, h * D // 2 + n, :] for n in range(D // 2)]
+                for n, term in enumerate(terms):
+                    nc.tensor.matmul(
+                        half[:, n % (D // 2)].rearrange("p s v j -> p (s v j)"),
+                        lhsT=term,
+                        rhs=ident[:],
+                        start=(n == 0),
+                        stop=(n == D - 1),
+                        is_transpose=True,
+                    )
+                others_ps.append(half)
+
+        def scale_half(a, h):
+            if h == 0:
+                z_bf[a] = ring.tile([P, P, PACK], BF16, name="z", align_bytes=64)
+            part = slice(h * D // 2, (h + 1) * D // 2)
+            factors = norm_sb[:, a * P : (a + 1) * P].rearrange("p (v d) -> p v d", d=D)[:, :, part]
             nc.vector.tensor_tensor(
-                others[:, a],
-                sums[pair][:, side].unsqueeze(2).to_broadcast([P, BASKETS, D, PACK]),
-                y_sb[pair][:, :, side].rearrange("p d v j -> p v d j"),
+                z_bf[a][:].rearrange("p (v d) j -> p v d j", d=D)[:, :, part],
+                others_ps[h][:, :, a % 2].rearrange("p d v j -> p v d j"),
+                factors.unsqueeze(3).to_broadcast([P, BASKETS, D // 2, PACK]),
+                ALU.mult,
+            )
+
+        def leave_out(a, first=0, count=BASKETS):
+            pair, side = divmod(a, 2)
+            baskets = slice(first, first + count)
+            nc.vector.tensor_tensor(
+                others[:, a, baskets],
+                sums[pair][:, side, baskets].unsqueeze(2).to_broadcast([P, count, D, PACK]),
+                y_sb[pair][:, :, side, baskets].rearrange("p d v j -> p v d j"),
                 ALU.subtract,
             )
 
@@ -177,7 +222,7 @@ def tile_picked_yfism_sig_p_kernel(
             )
             z_mx[a] = (z_codes[:], z_plane[:])
 
-        def score_turned(a, score_bank, turn_bank):
+        def score_turned(a, score_bank, turn_banks):
             scores = psum.tile([P, TILES, P], F32, name="scores_turned", tag=score_bank)
             for b in range(TILES):
                 targets = slice(b * P, (b + 1) * P)
@@ -185,12 +230,13 @@ def tile_picked_yfism_sig_p_kernel(
             probs = ring.tile([P, TILES, P], F32, name="probs", align_bytes=64)
             for b in range(TILES):
                 nc.scalar.activation(probs[:, b, :], scores[:, b, :], ACT.Sigmoid, bias=bias_cols[:, b : b + 1])
-            probs_back = psum.tile([P, TILES, P], F32, name="probs_back", tag=turn_bank)
-            for b in range(TILES):
-                nc.tensor.transpose(probs_back[:, b, :], probs[:, b, :], ident[:])
-            result = ring.tile([P, R], F32, name="result", align_bytes=64)
-            nc.scalar.copy(result[:], probs_back[:].rearrange("p b g -> p (b g)"))
-            nc.sync.dma_start(out=out[a * P : (a + 1) * P, :], in_=result[:])
+            for h, bank in enumerate(turn_banks):
+                probs_back = psum.tile([P, 2, P], F32, name="probs_back", tag=bank)
+                for n in range(2):
+                    nc.tensor.transpose(probs_back[:, n, :], probs[:, 2 * h + n, :], ident[:])
+                result = ring.tile([P, HALF], F32, name="result", align_bytes=64)
+                nc.scalar.copy(result[:], probs_back[:].rearrange("p b g -> p (b g)"))
+                nc.sync.dma_start(out=out[a * P : (a + 1) * P, h * HALF : (h + 1) * HALF], in_=result[:])
 
         def score_direct(a, h, bank, queue):
             targets = slice(h * HALF, (h + 1) * HALF)
@@ -207,42 +253,45 @@ def tile_picked_yfism_sig_p_kernel(
         basket_sums(0, "bank7", "bank5")
         project(2)
         project(3)
-        basket_sums(1, "bank4", "bank6")
-
         bias_picked = stage.tile([P, R], F32, name="bias_picked", align_bytes=64, offset=2 * W_BYTES)
         nc.vector.tensor_copy(bias_picked[:], bias_table[:].indirect(items_sb[:]))
         v_codes = keep.tile([P, R], U32, name="v_codes", tag="x_table", align_bytes=64)
         nc.vector.tensor_copy(v_codes[:], v_table[:].indirect(items_sb[:]))
         v_plane = keep.tile([P, R], U8, name="v_plane", tag="bias_table", align_bytes=64)
         nc.vector.tensor_copy(v_plane[:], v_table_scales[:].indirect(items_sb[:]))
-        others = keep.tile([P, TILES, BASKETS, D, PACK], F32, name="others", tag="v_table_scales", align_bytes=64)
+        others = keep.tile([P, 2, BASKETS, D, PACK], F32, name="others", tag="v_table_scales", align_bytes=64)
 
-        bias_turned = psum.tile([P, TILES, P], F32, name="bias_turned", tag="bank4")
+        bias_turned = psum.tile([P, TILES, P], F32, name="bias_turned", tag="bank7")
         for b in range(TILES):
             nc.tensor.transpose(bias_turned[:, b, :], bias_picked[:, b * P : (b + 1) * P], ident[:])
         bias_cols = keep.tile([P, TILES], F32, name="bias_cols")
         nc.scalar.copy(bias_cols[:], bias_turned[:, :, 0])
-        bias_spread = psum.tile([P, TILES, P], F32, name="bias_spread", tag="bank2")
+        turned_terms = turn_items(1, ("bank0", "bank1"), "bank4")
+        bias_spread = psum.tile([P, TILES, P], F32, name="bias_spread", tag="bank6")
         for b in range(TILES):
             nc.tensor.transpose(bias_spread[:, b, :], bias_cols[:, b : b + 1].to_broadcast([P, P]), ident[:])
         bias_rows = keep.tile([P, R], F32, name="bias_rows", align_bytes=64)
         nc.scalar.copy(bias_rows[:], bias_spread[:].rearrange("p b g -> p (b g)"))
 
+
         leave_out(0)
-        leave_out(1)
+        leave_out(1, 0, BASKETS // 2)
         scale_by_norm(0)
+        leave_out(1, BASKETS // 2, BASKETS // 2)
         quantize_z(0)
-        score_turned(0, "bank0", "bank3")
+        score_turned(0, "bank0", ("bank4", "bank6"))
+        turn_back(*turned_terms, ("bank2", "bank3"))
         scale_by_norm(1)
-        leave_out(2)
+        scale_half(2, 0)
         quantize_z(1)
-        score_turned(1, "bank1", "bank4")
-        scale_by_norm(2)
-        leave_out(3)
+        scale_half(3, 0)
+        scale_half(2, 1)
+        score_direct(1, 0, "bank1", nc.sync)
+        scale_half(3, 1)
         quantize_z(2)
-        scale_by_norm(3)
-        score_direct(2, 0, "bank7", nc.sync)
         quantize_z(3)
-        score_direct(2, 1, "bank2", nc.sync)
-        score_direct(3, 0, "bank5", nc.sync)
-        score_direct(3, 1, "bank6", nc.scalar)
+        score_direct(1, 1, "bank7", nc.sync)
+        score_direct(2, 0, "bank5", nc.sync)
+        score_direct(2, 1, "bank6", nc.sync)
+        score_direct(3, 0, "bank2", nc.sync)
+        score_direct(3, 1, "bank3", nc.scalar)

@@ -222,11 +222,14 @@ def tile_picked_yfism_sig_p_kernel(
             )
             z_mx[a] = (z_codes[:], z_plane[:])
 
-        def score_turned(a, score_bank, turn_banks):
+        def score_turned(a, score_bank):
             scores = psum.tile([P, TILES, P], F32, name="scores_turned", tag=score_bank)
             for b in range(TILES):
                 targets = slice(b * P, (b + 1) * P)
                 product(nc, scores[:, b, :], (v_codes[:, targets], v_plane[:, targets]), z_mx[a])
+            return scores
+
+        def finish_turned(a, scores, turn_banks):
             probs = ring.tile([P, TILES, P], F32, name="probs", align_bytes=64)
             for b in range(TILES):
                 nc.scalar.activation(probs[:, b, :], scores[:, b, :], ACT.Sigmoid, bias=bias_cols[:, b : b + 1])
@@ -279,8 +282,9 @@ def tile_picked_yfism_sig_p_kernel(
         scale_by_norm(0)
         leave_out(1, BASKETS // 2, BASKETS // 2)
         quantize_z(0)
-        score_turned(0, "bank0", ("bank4", "bank6"))
-        turn_back(*turned_terms, ("bank2", "bank3"))
+        scores_first = score_turned(0, "bank0")
+        turn_back(*turned_terms, ("bank2", "bank5"))
+        finish_turned(0, scores_first, ("bank4", "bank6"))
         scale_by_norm(1)
         scale_half(2, 0)
         quantize_z(1)
@@ -291,7 +295,7 @@ def tile_picked_yfism_sig_p_kernel(
         quantize_z(2)
         quantize_z(3)
         score_direct(1, 1, "bank7", nc.sync)
-        score_direct(2, 0, "bank5", nc.sync)
+        score_direct(2, 0, "bank3", nc.sync)
         score_direct(2, 1, "bank6", nc.sync)
         score_direct(3, 0, "bank2", nc.sync)
-        score_direct(3, 1, "bank3", nc.scalar)
+        score_direct(3, 1, "bank5", nc.scalar)

@@ -25,6 +25,7 @@ HALF = 256
 GROUPS = HALF // PACK
 CAST_SPLIT = 44
 LAST_CUT = 6
+WARM_PASSES = 4
 RING = 8
 W_BYTES = PACK * HALF * 4
 
@@ -256,6 +257,9 @@ def tile_picked_yfism_sig_p_kernel(
         basket_sums(0, "bank7", "bank5")
         project(2)
         project(3)
+        warm_ps = psum.tile([P, HALF], F32, name="warm_ps", tag="bank6")
+        for n in range(WARM_PASSES):
+            product(nc, warm_ps[:], (x_codes[0], x_plane[:, :P]), (picked[:], x_plane[:, HALF:]))
         bias_picked = stage.tile([P, R], F32, name="bias_picked", align_bytes=64, offset=2 * W_BYTES)
         nc.vector.tensor_copy(bias_picked[:], bias_table[:].indirect(items_sb[:]))
         v_codes = keep.tile([P, R], U32, name="v_codes", tag="x_table", align_bytes=64)

@@ -23,9 +23,7 @@ BASKETS = P // D
 LIST_COLS = P // 16
 HALF = 256
 GROUPS = HALF // PACK
-CAST_SPLIT = 44
-LAST_CUT = 6
-WARM_PASSES = 4
+W_FIRST = 384
 RING = 8
 W_BYTES = PACK * HALF * 4
 
@@ -65,13 +63,13 @@ def tile_picked_yfism_sig_p_kernel(
         items_sb = keep.tile([P, R // 16], U16, name="items_sb")
         x_table = keep.tile([P, T], U32, name="x_table", align_bytes=64)
         x_table_scales = keep.tile([P, T], U8, name="x_table_scales", align_bytes=64)
-        v_table = keep.tile([P, G], U32, name="v_table", align_bytes=64)
+        v_table = stage.tile([P, G], U32, name="v_table", align_bytes=64, offset=5 * W_BYTES)
         v_table_scales = keep.tile([P, G], U8, name="v_table_scales", align_bytes=64)
-        bias_table = keep.tile([P, G], F32, name="bias_table", align_bytes=64)
+        bias_table = stage.tile([P, G], F32, name="bias_table", align_bytes=64, offset=3 * W_BYTES)
         norm_sb = keep.tile([P, S], F32, name="norm_sb", align_bytes=64)
-        w_raw = [
-            stage.tile([P, PACK, HALF], F32, name="w_raw%d" % h, align_bytes=64, offset=W_BYTES * h) for h in range(2)
-        ]
+        w_first = stage.tile([P, PACK, W_FIRST], F32, name="w_first", align_bytes=64, offset=0)
+        w_rest = stage.tile([P, PACK, H - W_FIRST], F32, name="w_rest", align_bytes=64, offset=16 * W_FIRST)
+        v_plane = keep.tile([P, R], U8, name="v_plane", align_bytes=64)
         ident = keep.tile([P, P], F32, name="ident", align_bytes=64)
         warm_in = keep.tile([P, 1], F32, name="warm_in")
         warm_out = keep.tile([P, 1], F32, name="warm_out")
@@ -79,21 +77,28 @@ def tile_picked_yfism_sig_p_kernel(
         nc.gpsimd.memset(x_table_scales[:].bitcast(I32), 0)
         nc.gpsimd.memset(warm_in[:], 0.0)
         nc.scalar.activation(warm_out[:], warm_in[:], ACT.Sigmoid)
-        nc.gpsimd.memset(bias_table[:].bitcast(I32), 0)
-        nc.gpsimd.memset(v_table_scales[:].bitcast(I32), 0)
+        nc.gpsimd.memset(v_table_scales[: P - 16].bitcast(I32), 0)
+        nc.gpsimd.memset(v_plane[:].bitcast(I32), 0)
+        nc.vector.memset(bias_table[:].bitcast(I32), 0)
         make_identity(nc, ident[:])
 
-        w_rows = w1.rearrange("(p r) c -> p r c", r=PACK)
-        nc.sync.dma_start(out=w_raw[0][:], in_=w_rows[:, :, :HALF])
+        nc.sync.dma_start(items_sb[:], items)
+        nc.sync.dma_start(out=v_table_scales[P - 16 :].bitcast(I32), in_=v_scales[0].bitcast(I32))
         nc.sync.dma_start(offs_sb[:], offs)
         load_scale_rows(nc, x_table_scales, x_scales)
-        nc.sync.dma_start(out=w_raw[1][:], in_=w_rows[:, :, HALF:])
+        w_rows = w1.rearrange("(p r) c -> p r c", r=PACK)
+        nc.sync.dma_start(out=w_first[:], in_=w_rows[:, :, :W_FIRST])
+        nc.sync.dma_start(out=w_rest[:], in_=w_rows[:, :, W_FIRST:])
         load_words(nc, x_table, x_words)
-        nc.sync.dma_start(items_sb[:], items)
         nc.sync.dma_start(out=bias_table[0:1, :], in_=bias[0:1, :])
         load_words(nc, v_table, v_words)
-        load_scale_rows(nc, v_table_scales, v_scales)
         nc.sync.dma_start(out=norm_sb[:], in_=norm)
+
+        v_rows = keep.tile([P, R], U8, name="v_rows", align_bytes=64)
+        nc.vector.tensor_copy(v_rows[:], v_table_scales[:].indirect(items_sb[:]))
+        for q in range(4):
+            first = P - 16 + 4 * q
+            nc.sync.dma_start(out=v_plane[32 * q : 32 * q + 4].bitcast(I32), in_=v_rows[first : first + 4].bitcast(I32))
 
         x_plane = keep.tile([P, S], U8, name="x_plane", align_bytes=64)
         nc.vector.tensor_copy(x_plane[:], x_table_scales[:].indirect(offs_sb[:]))
@@ -101,146 +106,153 @@ def tile_picked_yfism_sig_p_kernel(
         w_grouped = stage.tile([P, PACK, P, PACK], BF16, name="w_grouped", align_bytes=64, offset=2 * W_BYTES)
         w_codes = keep.tile([P, PACK, P], U32, name="w_codes", align_bytes=64)
         w_plane = keep.tile([P, PACK, P], U8, name="w_plane", tag="x_table_scales", align_bytes=64)
-        for cast, h, lo, hi in (
-            (nc.scalar.copy, 0, 0, GROUPS),
-            (nc.vector.tensor_copy, 1, 0, CAST_SPLIT),
-            (nc.scalar.copy, 1, CAST_SPLIT, GROUPS),
-        ):
-            cast(
-                w_grouped[:, :, h * GROUPS + lo : h * GROUPS + hi, :].rearrange("p j m r -> p m j r"),
-                w_raw[h][:].rearrange("p r (m j) -> p m j r", j=PACK)[:, lo:hi],
-            )
-        nc.vector.quantize_mx(
-            out=w_codes[:].rearrange("p j m -> p (j m)").bitcast(FP8X4),
-            scales=w_plane[:].rearrange("p j m -> p (j m)"),
-            in_=w_grouped[:].rearrange("p j m r -> p (j m r)"),
-        )
-
+        for raw, first, split in ((w_first, 0, 60), (w_rest, W_FIRST // PACK, 20)):
+            groups = raw[:].rearrange("p r (m j) -> p m j r", j=PACK)
+            for cast, lo, hi in ((nc.vector.tensor_copy, 0, split), (nc.scalar.copy, split, groups.shape[1])):
+                cast(w_grouped[:, :, first + lo : first + hi, :].rearrange("p j m r -> p m j r"), groups[:, lo:hi])
         x_codes = []
-        for first, count in ((0, 1), (1, 1), (2, 2)):
-            picked = stage.tile(
-                [P, count * P], U32, name="x_codes%d" % first, align_bytes=64, offset=W_BYTES + 4 * P * first
-            )
+
+        def gather_x(first, count, offset):
+            picked = stage.tile([P, count * P], U32, name="x_codes%d" % first, align_bytes=64, offset=offset)
             entries = offs_sb[:, LIST_COLS * first : LIST_COLS * (first + count)]
             nc.vector.tensor_copy(picked[:], x_table[:].indirect(entries))
             x_codes.extend(picked[:, n * P : (n + 1) * P] for n in range(count))
 
-        sums, z_bf, z_mx, others_ps = {}, {}, {}, []
-        y_sb = [keep.tile([P, D, 2, BASKETS, PACK], F32, name="y_sb%d" % pair, align_bytes=64) for pair in range(2)]
+        for half in (slice(0, 2), slice(2, 4)):
+            if half.start:
+                gather_x(0, 1, 10 * W_BYTES)
+            nc.vector.quantize_mx(
+                out=w_codes[:, half].rearrange("p j m -> p (j m)").bitcast(FP8X4),
+                scales=w_plane[:, half].rearrange("p j m -> p (j m)"),
+                in_=w_grouped[:, half].rearrange("p j m r -> p (j m r)"),
+            )
+        gather_x(1, 1, 0)
+        gather_x(2, 2, 4 * P)
+
+        bias_picked = stage.tile([P, R], F32, name="bias_picked", align_bytes=64, offset=2 * W_BYTES - 4 * R)
+        nc.scalar.activation(bias_picked[:], bias_table[:].indirect(items_sb[:]), ACT.Copy)
+
+        y_ps, sums, others, z_bf, z_mx, others_ps = {}, {}, {}, {}, {}, []
+        y_sb = stage.tile([P, D, 2, BASKETS, PACK], F32, name="y_sb", align_bytes=64, offset=3 * W_BYTES)
+
+        rows = (slice(0, P), slice(P, 3 * P, 2), slice(P + 1, 3 * P, 2), slice(3 * P, 4 * P))
 
         def project(a):
-            y = psum.tile([P, PACK, P], F32, name="y", tag="bank%d" % a)
+            y_ps[a] = psum.tile([P, PACK, P], F32, name="y", tag="bank%d" % a)
             for j in range(PACK):
-                product(nc, y[:, j, :], (w_codes[:, j, :], w_plane[:, j, :]), (x_codes[a], x_plane[:, a * P : (a + 1) * P]))
-            pair, side = divmod(a, 2)
-            by_item = y[:].rearrange("p j (v d) -> p d v j", d=D)
-            cut = (D, D // 2, D, LAST_CUT)[a]
-            for part in (slice(0, cut), slice(cut, D)) if side else (slice(0, D),):
-                nc.scalar.copy(y_sb[pair][:, part, side], by_item[:, part])
-
-        def add_items(pair, adding_bank):
-            turned = psum.tile([P, P], F32, name="turned", tag=adding_bank)
-            for d in range(D):
-                nc.tensor.matmul(
-                    turned[:],
-                    lhsT=y_sb[pair][:, d].rearrange("p s v j -> p (s v j)"),
-                    rhs=ident[:],
-                    start=(d == 0),
-                    stop=(d == D - 1),
-                    is_transpose=True,
+                product(
+                    nc, y_ps[a][:, j, :], (w_codes[:, j, :], w_plane[:, j, :]), (x_codes[a], x_plane[:, a * P : (a + 1) * P])
                 )
-            turned_sb = ring.tile([P, P], F32, name="turned_sb", align_bytes=64)
-            nc.scalar.copy(turned_sb[:], turned[:])
-            return turned_sb
 
-        def basket_sums(pair, adding_bank, sums_bank):
-            turned_sb = add_items(pair, adding_bank)
-            sums[pair] = psum.tile([P, 2, BASKETS, PACK], F32, name="sums", tag=sums_bank)
-            nc.tensor.transpose(sums[pair][:].rearrange("p s v j -> p (s v j)"), turned_sb[:], ident[:])
+        def copy_out(a, parts):
+            by_item = y_ps[a][:].rearrange("p j (v d) -> p d v j", d=D)
+            for part in parts:
+                nc.scalar.copy(y_sb[:, part, a - 1], by_item[:, part])
 
-        def turn_items(pair, item_banks, adding_bank):
-            total = add_items(pair, adding_bank)
-            minus_y = keep.tile([P, D, P], F32, name="minus_y", align_bytes=64)
-            for h, bank in enumerate(item_banks):
-                items_turned = psum.tile([P, D // 2, P], F32, name="items_turned", tag=bank)
-                for n in range(D // 2):
-                    item = y_sb[pair][:, h * D // 2 + n].rearrange("p s v j -> p (s v j)")
-                    nc.tensor.transpose(items_turned[:, n, :], item, ident[:])
-                nc.scalar.activation(minus_y[:, h * D // 2 : (h + 1) * D // 2], items_turned[:], ACT.Copy, scale=-1.0)
-            return total, minus_y
+        def add_basket(a, offset, first=0, count=BASKETS):
+            sums[a, first] = stage.tile([P, count, PACK], F32, name="sums%d_%d" % (a, first), align_bytes=64, offset=offset)
+            by_basket = y_ps[a][:].rearrange("p j (v d) -> p v j d", d=D)
+            nc.vector.tensor_reduce(sums[a, first][:], by_basket[:, first : first + count], mybir.AxisListType.X, ALU.add)
 
-        def turn_back(total, minus_y, others_banks):
-            for h, bank in enumerate(others_banks):
-                half = psum.tile([P, D // 2, 2, BASKETS, PACK], F32, name="others_ps", tag=bank)
-                terms = [total[:]] * (D // 2) + [minus_y[:, h * D // 2 + n, :] for n in range(D // 2)]
-                for n, term in enumerate(terms):
-                    nc.tensor.matmul(
-                        half[:, n % (D // 2)].rearrange("p s v j -> p (s v j)"),
-                        lhsT=term,
-                        rhs=ident[:],
-                        start=(n == 0),
-                        stop=(n == D - 1),
-                        is_transpose=True,
-                    )
-                others_ps.append(half)
-
-        def scale_half(a, h):
-            if h == 0:
-                z_bf[a] = ring.tile([P, P, PACK], BF16, name="z", align_bytes=64)
-            part = slice(h * D // 2, (h + 1) * D // 2)
-            factors = norm_sb[:, a * P : (a + 1) * P].rearrange("p (v d) -> p v d", d=D)[:, :, part]
-            nc.vector.tensor_tensor(
-                z_bf[a][:].rearrange("p (v d) j -> p v d j", d=D)[:, :, part],
-                others_ps[h][:, :, a % 2].rearrange("p d v j -> p v d j"),
-                factors.unsqueeze(3).to_broadcast([P, BASKETS, D // 2, PACK]),
-                ALU.mult,
+        def leave_out(a, offset, first=0, count=BASKETS):
+            others[a, first] = stage.tile(
+                [P, count, D, PACK], F32, name="others%d_%d" % (a, first), align_bytes=64, offset=offset
             )
-
-        def leave_out(a, first=0, count=BASKETS):
-            pair, side = divmod(a, 2)
-            baskets = slice(first, first + count)
+            part = slice(first, first + count)
             nc.vector.tensor_tensor(
-                others[:, a, baskets],
-                sums[pair][:, side, baskets].unsqueeze(2).to_broadcast([P, count, D, PACK]),
-                y_sb[pair][:, :, side, baskets].rearrange("p d v j -> p v d j"),
+                others[a, first][:],
+                sums[a, 0][:, part].unsqueeze(2).to_broadcast([P, count, D, PACK]),
+                y_ps[a][:].rearrange("p j (v d) -> p v d j", d=D)[:, part],
                 ALU.subtract,
             )
 
-        def scale_by_norm(a):
-            z_bf[a] = ring.tile([P, P, PACK], BF16, name="z", align_bytes=64)
+        def scale_by_norm(a, offset, first=0, count=BASKETS):
+            if first == 0:
+                z_bf[a] = stage.tile([P, P, PACK], BF16, name="z%d" % a, align_bytes=64, offset=offset)
+            entries = slice(first * D, (first + count) * D)
             nc.vector.tensor_tensor(
-                z_bf[a][:],
-                others[:, a].rearrange("p v d j -> p (v d) j"),
-                norm_sb[:, a * P : (a + 1) * P].unsqueeze(2).to_broadcast([P, P, PACK]),
+                z_bf[a][:, entries],
+                others[a, first][:].rearrange("p v d j -> p (v d) j"),
+                norm_sb[:, a * P : (a + 1) * P][:, entries].unsqueeze(2).to_broadcast([P, count * D, PACK]),
+                ALU.mult,
+            )
+
+        def item(d):
+            return y_sb[:, d].rearrange("p s v j -> p (s v j)")
+
+        def negate_items(h, bank):
+            items_turned = psum.tile([P, D // 2, P], F32, name="items_turned", tag=bank)
+            for n in range(D // 2):
+                nc.tensor.transpose(items_turned[:, n, :], item(2 * n + h), ident[:])
+            minus_y = stage.tile([P, D // 2, P], F32, name="minus_y%d" % h, align_bytes=64, offset=(7 + h) * W_BYTES)
+            nc.scalar.activation(minus_y[:], items_turned[:], ACT.Copy, scale=-1.0)
+            return minus_y
+
+        def add_items(bank):
+            turned = psum.tile([P, P], F32, name="turned", tag=bank)
+            for n in range(D):
+                d = 2 * n % D + 2 * n // D
+                nc.tensor.matmul(turned[:], lhsT=item(d), rhs=ident[:], start=(n == 0), stop=(n == D - 1), is_transpose=True)
+            total = keep.tile([P, P], F32, name="total", align_bytes=64)
+            nc.scalar.copy(total[:], turned[:])
+            return total
+
+        def turn_back(total, minus_y, bank):
+            half = psum.tile([P, D // 2, 2, BASKETS, PACK], F32, name="others_ps", tag=bank)
+            terms = [minus_y[:, n, :] for n in range(D // 2)] + [total[:]] * (D // 2)
+            for n, term in enumerate(terms):
+                nc.tensor.matmul(
+                    half[:, n % (D // 2)].rearrange("p s v j -> p (s v j)"),
+                    lhsT=term,
+                    rhs=ident[:],
+                    start=(n == 0),
+                    stop=(n == D - 1),
+                    is_transpose=True,
+                )
+            others_ps.append(half)
+
+        def scale_bank(h):
+            z_bf[1 + h] = ring.tile([P, P, PACK], BF16, name="z", align_bytes=64)
+            factors = norm_sb[:, P : 3 * P].rearrange("p (v d) -> p v d", d=D)[:, :, h::2]
+            nc.vector.tensor_tensor(
+                z_bf[1 + h][:].rearrange("p (v n) j -> p v n j", n=D // 2),
+                others_ps[h][:].rearrange("p n s v j -> p (s v) n j"),
+                factors.unsqueeze(3).to_broadcast([P, 2 * BASKETS, D // 2, PACK]),
                 ALU.mult,
             )
 
         def quantize_z(a):
             z_codes = ring.tile([P, P], U32, name="z_codes", align_bytes=64)
-            z_plane = ring.tile([P, P], U8, name="z_plane", align_bytes=64)
+            if a == 0:
+                z_plane = stage.tile([P, P], U8, name="z_plane0", align_bytes=64, offset=7 * W_BYTES)
+            else:
+                z_plane = ring.tile([P, P], U8, name="z_plane", align_bytes=64)
             nc.vector.quantize_mx(
                 out=z_codes[:].bitcast(FP8X4), scales=z_plane[:], in_=z_bf[a][:].rearrange("p t j -> p (t j)")
             )
             z_mx[a] = (z_codes[:], z_plane[:])
 
-        def score_turned(a, score_bank):
-            scores = psum.tile([P, TILES, P], F32, name="scores_turned", tag=score_bank)
-            for b in range(TILES):
+        def score_turned(a, score_bank, blocks=TILES):
+            scores = psum.tile([P, blocks, P], F32, name="scores_turned", tag=score_bank)
+            for b in range(blocks):
                 targets = slice(b * P, (b + 1) * P)
                 product(nc, scores[:, b, :], (v_codes[:, targets], v_plane[:, targets]), z_mx[a])
             return scores
 
-        def finish_turned(a, scores, turn_banks):
+        def squash_turned(scores):
             probs = ring.tile([P, TILES, P], F32, name="probs", align_bytes=64)
-            for b in range(TILES):
+            for b in range(scores.shape[1]):
                 nc.scalar.activation(probs[:, b, :], scores[:, b, :], ACT.Sigmoid, bias=bias_cols[:, b : b + 1])
+            return probs
+
+        def finish_turned(a, probs, turn_banks):
             for h, bank in enumerate(turn_banks):
                 probs_back = psum.tile([P, 2, P], F32, name="probs_back", tag=bank)
                 for n in range(2):
                     nc.tensor.transpose(probs_back[:, n, :], probs[:, 2 * h + n, :], ident[:])
                 result = ring.tile([P, HALF], F32, name="result", align_bytes=64)
                 nc.scalar.copy(result[:], probs_back[:].rearrange("p b g -> p (b g)"))
-                nc.sync.dma_start(out=out[a * P : (a + 1) * P, h * HALF : (h + 1) * HALF], in_=result[:])
+                nc.sync.dma_start(out=out[rows[a], h * HALF : (h + 1) * HALF], in_=result[:])
 
         def score_direct(a, h, bank, queue):
             targets = slice(h * HALF, (h + 1) * HALF)
@@ -250,56 +262,56 @@ def tile_picked_yfism_sig_p_kernel(
             nc.vector.tensor_tensor(logits[:], scores[:], bias_rows[:, targets], ALU.add)
             result = ring.tile([P, HALF], F32, name="result", align_bytes=64)
             nc.scalar.activation(result[:], logits[:], ACT.Sigmoid)
-            queue.dma_start(out=out[a * P : (a + 1) * P, targets], in_=result[:])
+            queue.dma_start(out=out[rows[a], targets], in_=result[:])
 
-        project(0)
-        project(1)
-        basket_sums(0, "bank7", "bank5")
-        project(2)
-        project(3)
         warm_ps = psum.tile([P, HALF], F32, name="warm_ps", tag="bank6")
-        for n in range(WARM_PASSES):
-            product(nc, warm_ps[:], (x_codes[0], x_plane[:, :P]), (picked[:], x_plane[:, HALF:]))
-        bias_picked = stage.tile([P, R], F32, name="bias_picked", align_bytes=64, offset=2 * W_BYTES)
-        nc.vector.tensor_copy(bias_picked[:], bias_table[:].indirect(items_sb[:]))
-        v_codes = keep.tile([P, R], U32, name="v_codes", tag="x_table", align_bytes=64)
-        nc.vector.tensor_copy(v_codes[:], v_table[:].indirect(items_sb[:]))
-        v_plane = keep.tile([P, R], U8, name="v_plane", tag="bias_table", align_bytes=64)
-        nc.vector.tensor_copy(v_plane[:], v_table_scales[:].indirect(items_sb[:]))
-        others = keep.tile([P, 2, BASKETS, D, PACK], F32, name="others", tag="v_table_scales", align_bytes=64)
-
+        warm_moving = (w_codes[:, :2].rearrange("p j m -> p (j m)"), w_plane[:, :2].rearrange("p j m -> p (j m)"))
+        for n in range(2):
+            product(nc, warm_ps[:], (w_codes[:, 0, :], w_plane[:, 0, :]), warm_moving)
+        for a in range(TILES):
+            project(a)
+        late_ps = psum.tile([P, HALF], F32, name="late_ps", tag="bank6")
+        for n in range(2):
+            product(nc, late_ps[:], (x_codes[3], x_plane[:, 3 * P :]), warm_moving)
+        copy_out(1, (slice(0, D),))
+        copy_out(2, (slice(0, D, 2), slice(1, D, 2)))
+        add_basket(0, 4 * W_BYTES)
+        leave_out(0, 9 * W_BYTES)
         bias_turned = psum.tile([P, TILES, P], F32, name="bias_turned", tag="bank7")
         for b in range(TILES):
             nc.tensor.transpose(bias_turned[:, b, :], bias_picked[:, b * P : (b + 1) * P], ident[:])
         bias_cols = keep.tile([P, TILES], F32, name="bias_cols")
         nc.scalar.copy(bias_cols[:], bias_turned[:, :, 0])
-        turned_terms = turn_items(1, ("bank0", "bank1"), "bank4")
-        bias_spread = psum.tile([P, TILES, P], F32, name="bias_spread", tag="bank6")
+        minus_even = negate_items(0, "bank1")
+        total = add_items("bank4")
+        minus_odd = negate_items(1, "bank2")
+        v_codes = keep.tile([P, R], U32, name="v_codes", align_bytes=64)
+        nc.vector.tensor_copy(v_codes[:], v_table[:].indirect(items_sb[:]))
+        scale_by_norm(0, 11 * W_BYTES)
+        add_basket(3, 3 * W_BYTES)
+        leave_out(3, 12 * W_BYTES, 0, BASKETS // 2)
+        turn_back(total, minus_even, "bank5")
+        quantize_z(0)
+        scores0 = score_turned(0, "bank0")
+        turn_back(total, minus_odd, "bank6")
+        bias_spread = psum.tile([P, TILES, P], F32, name="bias_spread", tag="bank2")
         for b in range(TILES):
             nc.tensor.transpose(bias_spread[:, b, :], bias_cols[:, b : b + 1].to_broadcast([P, P]), ident[:])
+        probs0 = squash_turned(scores0)
         bias_rows = keep.tile([P, R], F32, name="bias_rows", align_bytes=64)
         nc.scalar.copy(bias_rows[:], bias_spread[:].rearrange("p b g -> p (b g)"))
-
-
-        leave_out(0)
-        leave_out(1, 0, BASKETS // 2)
-        scale_by_norm(0)
-        leave_out(1, BASKETS // 2, BASKETS // 2)
-        quantize_z(0)
-        scores_first = score_turned(0, "bank0")
-        turn_back(*turned_terms, ("bank2", "bank5"))
-        finish_turned(0, scores_first, ("bank4", "bank6"))
-        scale_by_norm(1)
-        scale_half(2, 0)
+        finish_turned(0, probs0, ("bank4", "bank1"))
+        scale_bank(0)
+        leave_out(3, 7 * W_BYTES + 9 * P, BASKETS // 2, BASKETS // 2)
         quantize_z(1)
-        scale_half(3, 0)
-        scale_half(2, 1)
-        score_direct(1, 0, "bank1", nc.sync)
-        scale_half(3, 1)
+        scale_by_norm(3, 7 * W_BYTES + P, 0, BASKETS // 2)
+        scale_bank(1)
+        scale_by_norm(3, 7 * W_BYTES + P, BASKETS // 2, BASKETS // 2)
+        score_direct(1, 0, "bank7", nc.sync)
         quantize_z(2)
+        score_direct(1, 1, "bank5", nc.sync)
         quantize_z(3)
-        score_direct(1, 1, "bank7", nc.sync)
-        score_direct(2, 0, "bank3", nc.sync)
-        score_direct(2, 1, "bank6", nc.sync)
-        score_direct(3, 0, "bank2", nc.sync)
-        score_direct(3, 1, "bank5", nc.scalar)
+        score_direct(2, 0, "bank0", nc.sync)
+        score_direct(2, 1, "bank2", nc.sync)
+        score_direct(3, 0, "bank3", nc.sync)
+        score_direct(3, 1, "bank6", nc.scalar)

@@ -110,23 +110,24 @@ def tile_picked_yfism_sig_p_kernel(
             groups = raw[:].rearrange("p r (m j) -> p m j r", j=PACK)
             for cast, lo, hi in ((nc.vector.tensor_copy, 0, split), (nc.scalar.copy, split, groups.shape[1])):
                 cast(w_grouped[:, :, first + lo : first + hi, :].rearrange("p j m r -> p m j r"), groups[:, lo:hi])
-        x_codes = []
+        x_codes = {}
 
         def gather_x(first, count, offset):
             picked = stage.tile([P, count * P], U32, name="x_codes%d" % first, align_bytes=64, offset=offset)
             entries = offs_sb[:, LIST_COLS * first : LIST_COLS * (first + count)]
             nc.vector.tensor_copy(picked[:], x_table[:].indirect(entries))
-            x_codes.extend(picked[:, n * P : (n + 1) * P] for n in range(count))
+            for n in range(count):
+                x_codes[first + n] = picked[:, n * P : (n + 1) * P]
 
         for half in (slice(0, 2), slice(2, 4)):
             if half.start:
-                gather_x(0, 1, 10 * W_BYTES)
+                gather_x(1, 1, 10 * W_BYTES)
             nc.vector.quantize_mx(
                 out=w_codes[:, half].rearrange("p j m -> p (j m)").bitcast(FP8X4),
                 scales=w_plane[:, half].rearrange("p j m -> p (j m)"),
                 in_=w_grouped[:, half].rearrange("p j m r -> p (j m r)"),
             )
-        gather_x(1, 1, 0)
+        gather_x(0, 1, 0)
         gather_x(2, 2, 4 * P)
 
         bias_picked = stage.tile([P, R], F32, name="bias_picked", align_bytes=64, offset=2 * W_BYTES - 4 * R)
@@ -268,15 +269,31 @@ def tile_picked_yfism_sig_p_kernel(
         warm_moving = (w_codes[:, :2].rearrange("p j m -> p (j m)"), w_plane[:, :2].rearrange("p j m -> p (j m)"))
         for n in range(2):
             product(nc, warm_ps[:], (w_codes[:, 0, :], w_plane[:, 0, :]), warm_moving)
-        for a in range(TILES):
+        project(1)
+        first_ps = []
+        for bank in ("bank0", "bank5"):
+            half = psum.tile([P, 2, P], F32, name="first_ps", tag=bank)
+            for n in range(2):
+                j = 2 * len(first_ps) + n
+                product(nc, half[:, n, :], (w_codes[:, j, :], w_plane[:, j, :]), (x_codes[0], x_plane[:, :P]))
+            first_ps.append(half)
+        for a in range(2, TILES):
             project(a)
-        late_ps = psum.tile([P, HALF], F32, name="late_ps", tag="bank6")
-        for n in range(2):
-            product(nc, late_ps[:], (x_codes[3], x_plane[:, 3 * P :]), warm_moving)
         copy_out(1, (slice(0, D),))
         copy_out(2, (slice(0, D, 2), slice(1, D, 2)))
-        add_basket(0, 4 * W_BYTES)
-        leave_out(0, 9 * W_BYTES)
+        first_sums = keep.tile([P, 2, BASKETS, 2], F32, name="first_sums", align_bytes=64)
+        first_others = keep.tile([P, 2, BASKETS, D, 2], F32, name="first_others", align_bytes=64)
+        for u in range(2):
+            nc.vector.tensor_reduce(
+                first_sums[:, u], first_ps[u][:].rearrange("p j (v d) -> p v j d", d=D), mybir.AxisListType.X, ALU.add
+            )
+        for u in range(2):
+            nc.vector.tensor_tensor(
+                first_others[:, u],
+                first_sums[:, u].unsqueeze(2).to_broadcast([P, BASKETS, D, 2]),
+                first_ps[u][:].rearrange("p j (v d) -> p v d j", d=D),
+                ALU.subtract,
+            )
         bias_turned = psum.tile([P, TILES, P], F32, name="bias_turned", tag="bank7")
         for b in range(TILES):
             nc.tensor.transpose(bias_turned[:, b, :], bias_picked[:, b * P : (b + 1) * P], ident[:])
@@ -287,9 +304,15 @@ def tile_picked_yfism_sig_p_kernel(
         minus_odd = negate_items(1, "bank2")
         v_codes = keep.tile([P, R], U32, name="v_codes", align_bytes=64)
         nc.vector.tensor_copy(v_codes[:], v_table[:].indirect(items_sb[:]))
-        scale_by_norm(0, 11 * W_BYTES)
+        z_bf[0] = keep.tile([P, P, PACK], BF16, name="z0", align_bytes=64)
+        nc.vector.tensor_tensor(
+            z_bf[0][:].rearrange("p t (u j) -> p t u j", u=2),
+            first_others[:].rearrange("p u v d j -> p (v d) u j"),
+            norm_sb[:, :P].unsqueeze(2).unsqueeze(3).to_broadcast([P, P, 2, 2]),
+            ALU.mult,
+        )
         add_basket(3, 3 * W_BYTES)
-        leave_out(3, 12 * W_BYTES, 0, BASKETS // 2)
+        leave_out(3, 12 * W_BYTES)
         turn_back(total, minus_even, "bank5")
         quantize_z(0)
         scores0 = score_turned(0, "bank0")
@@ -302,16 +325,14 @@ def tile_picked_yfism_sig_p_kernel(
         nc.scalar.copy(bias_rows[:], bias_spread[:].rearrange("p b g -> p (b g)"))
         finish_turned(0, probs0, ("bank4", "bank1"))
         scale_bank(0)
-        leave_out(3, 7 * W_BYTES + 9 * P, BASKETS // 2, BASKETS // 2)
+        scale_by_norm(3, 7 * W_BYTES + P)
         quantize_z(1)
-        scale_by_norm(3, 7 * W_BYTES + P, 0, BASKETS // 2)
         scale_bank(1)
-        scale_by_norm(3, 7 * W_BYTES + P, BASKETS // 2, BASKETS // 2)
+        quantize_z(3)
         score_direct(1, 0, "bank7", nc.sync)
         quantize_z(2)
         score_direct(1, 1, "bank5", nc.sync)
-        quantize_z(3)
-        score_direct(2, 0, "bank0", nc.sync)
-        score_direct(2, 1, "bank2", nc.sync)
         score_direct(3, 0, "bank3", nc.sync)
-        score_direct(3, 1, "bank6", nc.scalar)
+        score_direct(3, 1, "bank0", nc.sync)
+        score_direct(2, 0, "bank2", nc.sync)
+        score_direct(2, 1, "bank6", nc.scalar)

@@ -314,15 +314,15 @@ def tile_picked_yfism_sig_p_kernel(
         add_basket(3, 3 * W_BYTES)
         leave_out(3, 12 * W_BYTES)
         turn_back(total, minus_even, "bank5")
+        bias_spread = psum.tile([P, TILES, P], F32, name="bias_spread", tag="bank1")
+        for b in range(TILES):
+            nc.tensor.transpose(bias_spread[:, b, :], bias_cols[:, b : b + 1].to_broadcast([P, P]), ident[:])
+        bias_rows = keep.tile([P, R], F32, name="bias_rows", align_bytes=64)
+        nc.scalar.copy(bias_rows[:], bias_spread[:].rearrange("p b g -> p (b g)"))
         quantize_z(0)
         scores0 = score_turned(0, "bank0")
         turn_back(total, minus_odd, "bank6")
-        bias_spread = psum.tile([P, TILES, P], F32, name="bias_spread", tag="bank2")
-        for b in range(TILES):
-            nc.tensor.transpose(bias_spread[:, b, :], bias_cols[:, b : b + 1].to_broadcast([P, P]), ident[:])
         probs0 = squash_turned(scores0)
-        bias_rows = keep.tile([P, R], F32, name="bias_rows", align_bytes=64)
-        nc.scalar.copy(bias_rows[:], bias_spread[:].rearrange("p b g -> p (b g)"))
         finish_turned(0, probs0, ("bank4", "bank1"))
         scale_bank(0)
         scale_by_norm(3, 7 * W_BYTES + P)

@@ -23,7 +23,7 @@ BASKETS = P // D
 LIST_COLS = P // 16
 HALF = 256
 GROUPS = HALF // PACK
-W_FIRST = 384
+W_FIRST = 320
 RING = 8
 W_BYTES = PACK * HALF * 4
 
@@ -106,7 +106,7 @@ def tile_picked_yfism_sig_p_kernel(
         w_grouped = stage.tile([P, PACK, P, PACK], BF16, name="w_grouped", align_bytes=64, offset=2 * W_BYTES)
         w_codes = keep.tile([P, PACK, P], U32, name="w_codes", align_bytes=64)
         w_plane = keep.tile([P, PACK, P], U8, name="w_plane", tag="x_table_scales", align_bytes=64)
-        for raw, first, split in ((w_first, 0, 60), (w_rest, W_FIRST // PACK, 20)):
+        for raw, first, split in ((w_first, 0, 44), (w_rest, W_FIRST // PACK, 30)):
             groups = raw[:].rearrange("p r (m j) -> p m j r", j=PACK)
             for cast, lo, hi in ((nc.vector.tensor_copy, 0, split), (nc.scalar.copy, split, groups.shape[1])):
                 cast(w_grouped[:, :, first + lo : first + hi, :].rearrange("p j m r -> p m j r"), groups[:, lo:hi])
@@ -134,7 +134,10 @@ def tile_picked_yfism_sig_p_kernel(
         nc.scalar.activation(bias_picked[:], bias_table[:].indirect(items_sb[:]), ACT.Copy)
 
         y_ps, sums, others, z_bf, z_mx, others_ps = {}, {}, {}, {}, {}, []
-        y_sb = stage.tile([P, D, 2, BASKETS, PACK], F32, name="y_sb", align_bytes=64, offset=3 * W_BYTES)
+        y_sb = [
+            stage.tile([P, D // 2, 2, BASKETS, PACK], F32, name="y_sb%d" % h, align_bytes=64, offset=(6 + h) * W_BYTES // 2)
+            for h in range(2)
+        ]
 
         rows = (slice(0, P), slice(P, 3 * P, 2), slice(P + 1, 3 * P, 2), slice(3 * P, 4 * P))
 
@@ -145,23 +148,22 @@ def tile_picked_yfism_sig_p_kernel(
                     nc, y_ps[a][:, j, :], (w_codes[:, j, :], w_plane[:, j, :]), (x_codes[a], x_plane[:, a * P : (a + 1) * P])
                 )
 
-        def copy_out(a, parts):
-            by_item = y_ps[a][:].rearrange("p j (v d) -> p d v j", d=D)
-            for part in parts:
-                nc.scalar.copy(y_sb[:, part, a - 1], by_item[:, part])
+        def copy_out(a, h):
+            nc.scalar.copy(y_sb[h][:, :, a - 1], y_ps[a][:].rearrange("p j (v d) -> p d v j", d=D)[:, h::2])
 
         def add_basket(a, offset, first=0, count=BASKETS):
-            sums[a, first] = stage.tile([P, count, PACK], F32, name="sums%d_%d" % (a, first), align_bytes=64, offset=offset)
+            if first == 0:
+                sums[a, 0] = stage.tile([P, BASKETS, PACK], F32, name="sums%d" % a, align_bytes=64, offset=offset)
+            part = slice(first, first + count)
             by_basket = y_ps[a][:].rearrange("p j (v d) -> p v j d", d=D)
-            nc.vector.tensor_reduce(sums[a, first][:], by_basket[:, first : first + count], mybir.AxisListType.X, ALU.add)
+            nc.vector.tensor_reduce(sums[a, 0][:, part], by_basket[:, part], mybir.AxisListType.X, ALU.add)
 
         def leave_out(a, offset, first=0, count=BASKETS):
-            others[a, first] = stage.tile(
-                [P, count, D, PACK], F32, name="others%d_%d" % (a, first), align_bytes=64, offset=offset
-            )
+            if first == 0:
+                others[a, 0] = stage.tile([P, BASKETS, D, PACK], F32, name="others%d" % a, align_bytes=64, offset=offset)
             part = slice(first, first + count)
             nc.vector.tensor_tensor(
-                others[a, first][:],
+                others[a, 0][:, part],
                 sums[a, 0][:, part].unsqueeze(2).to_broadcast([P, count, D, PACK]),
                 y_ps[a][:].rearrange("p j (v d) -> p v d j", d=D)[:, part],
                 ALU.subtract,
@@ -179,7 +181,7 @@ def tile_picked_yfism_sig_p_kernel(
             )
 
         def item(d):
-            return y_sb[:, d].rearrange("p s v j -> p (s v j)")
+            return y_sb[d % 2][:, d // 2].rearrange("p s v j -> p (s v j)")
 
         def negate_items(h, bank):
             items_turned = psum.tile([P, D // 2, P], F32, name="items_turned", tag=bank)
@@ -255,20 +257,23 @@ def tile_picked_yfism_sig_p_kernel(
                 nc.scalar.copy(result[:], probs_back[:].rearrange("p b g -> p (b g)"))
                 nc.sync.dma_start(out=out[rows[a], h * HALF : (h + 1) * HALF], in_=result[:])
 
-        def score_direct(a, h, bank, queue):
+        def score_half(a, h, bank):
             targets = slice(h * HALF, (h + 1) * HALF)
             scores = psum.tile([P, HALF], F32, name="scores_direct", tag=bank)
             product(nc, scores[:], z_mx[a], (v_codes[:, targets], v_plane[:, targets]))
+            return scores
+
+        def finish_half(a, h, scores, queue):
+            targets = slice(h * HALF, (h + 1) * HALF)
             logits = ring.tile([P, HALF], F32, name="logits", align_bytes=64)
             nc.vector.tensor_tensor(logits[:], scores[:], bias_rows[:, targets], ALU.add)
             result = ring.tile([P, HALF], F32, name="result", align_bytes=64)
             nc.scalar.activation(result[:], logits[:], ACT.Sigmoid)
             queue.dma_start(out=out[rows[a], targets], in_=result[:])
 
-        warm_ps = psum.tile([P, HALF], F32, name="warm_ps", tag="bank6")
-        warm_moving = (w_codes[:, :2].rearrange("p j m -> p (j m)"), w_plane[:, :2].rearrange("p j m -> p (j m)"))
-        for n in range(2):
-            product(nc, warm_ps[:], (w_codes[:, 0, :], w_plane[:, 0, :]), warm_moving)
+        def score_direct(a, h, bank, queue):
+            finish_half(a, h, score_half(a, h, bank), queue)
+
         project(1)
         first_ps = []
         for bank in ("bank0", "bank5"):
@@ -279,8 +284,9 @@ def tile_picked_yfism_sig_p_kernel(
             first_ps.append(half)
         for a in range(2, TILES):
             project(a)
-        copy_out(1, (slice(0, D),))
-        copy_out(2, (slice(0, D, 2), slice(1, D, 2)))
+        for a in (1, 2):
+            for h in range(2):
+                copy_out(a, h)
         first_sums = keep.tile([P, 2, BASKETS, 2], F32, name="first_sums", align_bytes=64)
         first_others = keep.tile([P, 2, BASKETS, D, 2], F32, name="first_others", align_bytes=64)
         for u in range(2):
@@ -294,6 +300,10 @@ def tile_picked_yfism_sig_p_kernel(
                 first_ps[u][:].rearrange("p j (v d) -> p v d j", d=D),
                 ALU.subtract,
             )
+        for first in (0, BASKETS // 2):
+            add_basket(3, 13 * W_BYTES, first, BASKETS // 2)
+        for first in (0, BASKETS // 2):
+            leave_out(3, 12 * W_BYTES, first, BASKETS // 2)
         bias_turned = psum.tile([P, TILES, P], F32, name="bias_turned", tag="bank7")
         for b in range(TILES):
             nc.tensor.transpose(bias_turned[:, b, :], bias_picked[:, b * P : (b + 1) * P], ident[:])
@@ -305,14 +315,12 @@ def tile_picked_yfism_sig_p_kernel(
         v_codes = keep.tile([P, R], U32, name="v_codes", align_bytes=64)
         nc.vector.tensor_copy(v_codes[:], v_table[:].indirect(items_sb[:]))
         z_bf[0] = keep.tile([P, P, PACK], BF16, name="z0", align_bytes=64)
-        nc.vector.tensor_tensor(
+        nc.gpsimd.tensor_tensor(
             z_bf[0][:].rearrange("p t (u j) -> p t u j", u=2),
             first_others[:].rearrange("p u v d j -> p (v d) u j"),
             norm_sb[:, :P].unsqueeze(2).unsqueeze(3).to_broadcast([P, P, 2, 2]),
             ALU.mult,
         )
-        add_basket(3, 3 * W_BYTES)
-        leave_out(3, 12 * W_BYTES)
         turn_back(total, minus_even, "bank5")
         bias_spread = psum.tile([P, TILES, P], F32, name="bias_spread", tag="bank1")
         for b in range(TILES):
@@ -320,16 +328,18 @@ def tile_picked_yfism_sig_p_kernel(
         bias_rows = keep.tile([P, R], F32, name="bias_rows", align_bytes=64)
         nc.scalar.copy(bias_rows[:], bias_spread[:].rearrange("p b g -> p (b g)"))
         quantize_z(0)
-        scores0 = score_turned(0, "bank0")
+        scores0 = score_turned(0, "bank0", 2)
+        scores0_direct = score_half(0, 1, "bank7")
         turn_back(total, minus_odd, "bank6")
         probs0 = squash_turned(scores0)
-        finish_turned(0, probs0, ("bank4", "bank1"))
+        finish_turned(0, probs0, ("bank4",))
         scale_bank(0)
         scale_by_norm(3, 7 * W_BYTES + P)
         quantize_z(1)
+        finish_half(0, 1, scores0_direct, nc.sync)
         scale_bank(1)
         quantize_z(3)
-        score_direct(1, 0, "bank7", nc.sync)
+        score_direct(1, 0, "bank1", nc.sync)
         quantize_z(2)
         score_direct(1, 1, "bank5", nc.sync)
         score_direct(3, 0, "bank3", nc.sync)

from contextlib import ExitStack

import concourse.mybir as mybir
from concourse.masks import make_identity

K, T, S, D, H, G, R = 512, 1024, 512, 8, 512, 2048, 512
FLOPS = 2 * K * H * S + 2 * H * S * R

F32 = mybir.dt.float32
BF16 = mybir.dt.bfloat16
I32 = mybir.dt.int32
U32 = mybir.dt.uint32
U16 = mybir.dt.uint16
U8 = mybir.dt.uint8
FP8X4 = mybir.dt.float8_e4m3fn_x4
ALU = mybir.AluOpType
ACT = mybir.ActivationFunctionType

P = 128
PACK = 4
TILES = S // P
BASKETS = P // D
LIST_COLS = P // 16
HALF = 256
GROUPS = HALF // PACK
W_FIRST = 320
RING = 8
W_BYTES = PACK * HALF * 4


def load_scale_rows(nc, plane, rows):
    for r in range(4):
        nc.sync.dma_start(out=plane[r:P:32, :].bitcast(I32), in_=rows[0, r:16:4, :].bitcast(I32))


def load_words(nc, table, words):
    nc.sync.dma_start(out=table[:].bitcast(I32), in_=words[0].rearrange("p n r -> p (n r)").bitcast(I32))


def product(nc, acc, stationary, moving):
    nc.tensor.matmul_mx(
        out=acc,
        lhsT=stationary[0].bitcast(FP8X4),
        lhsT_scale=stationary[1],
        rhs=moving[0].bitcast(FP8X4),
        rhs_scale=moving[1],
        start=True,
        stop=True,
    )


def tile_picked_yfism_sig_p_kernel(
    tc, x_words, x_scales, w1, norm, v_words, v_scales, bias, offs, items, out
):
    nc = tc.nc
    with ExitStack() as ctx:
        keep = ctx.enter_context(tc.tile_pool(name="keep", bufs=1))
        stage = ctx.enter_context(tc.tile_pool(name="stage", bufs=1))
        ring = ctx.enter_context(tc.tile_pool(name="ring", bufs=RING))
        psum = ctx.enter_context(tc.psum_pool(name="psum", bufs=1))

        offs_sb = keep.tile([P, S // 16], U16, name="offs_sb")
        items_sb = keep.tile([P, R // 16], U16, name="items_sb")
        x_table = keep.tile([P, T], U32, name="x_table", align_bytes=64)
        x_table_scales = keep.tile([P, T], U8, name="x_table_scales", align_bytes=64)
        v_table = stage.tile([P, G], U32, name="v_table", align_bytes=64, offset=5 * W_BYTES)
        v_table_scales = keep.tile([P, G], U8, name="v_table_scales", align_bytes=64)
        bias_table = stage.tile([P, G], F32, name="bias_table", align_bytes=64, offset=3 * W_BYTES)
        norm_sb = keep.tile([P, S], F32, name="norm_sb", align_bytes=64)
        w_first = stage.tile([P, PACK, W_FIRST], F32, name="w_first", align_bytes=64, offset=0)
        w_rest = stage.tile([P, PACK, H - W_FIRST], F32, name="w_rest", align_bytes=64, offset=16 * W_FIRST)
        v_plane = keep.tile([P, R], U8, name="v_plane", align_bytes=64)
        ident = keep.tile([P, P], F32, name="ident", align_bytes=64)
        warm_in = keep.tile([P, 1], F32, name="warm_in")
        warm_out = keep.tile([P, 1], F32, name="warm_out")

        nc.gpsimd.memset(x_table_scales[:].bitcast(I32), 0)
        nc.gpsimd.memset(warm_in[:], 0.0)
        nc.scalar.activation(warm_out[:], warm_in[:], ACT.Sigmoid)
        nc.gpsimd.memset(v_table_scales[: P - 16].bitcast(I32), 0)
        nc.gpsimd.memset(v_plane[:].bitcast(I32), 0)
        nc.vector.memset(bias_table[:].bitcast(I32), 0)
        make_identity(nc, ident[:])

        nc.sync.dma_start(items_sb[:], items)
        nc.sync.dma_start(out=v_table_scales[P - 16 :].bitcast(I32), in_=v_scales[0].bitcast(I32))
        nc.sync.dma_start(offs_sb[:], offs)
        load_scale_rows(nc, x_table_scales, x_scales)
        w_rows = w1.rearrange("(p r) c -> p r c", r=PACK)
        nc.sync.dma_start(out=w_first[:], in_=w_rows[:, :, :W_FIRST])
        nc.sync.dma_start(out=w_rest[:], in_=w_rows[:, :, W_FIRST:])
        load_words(nc, x_table, x_words)
        nc.sync.dma_start(out=bias_table[0:1, :], in_=bias[0:1, :])
        load_words(nc, v_table, v_words)
        nc.sync.dma_start(out=norm_sb[:], in_=norm)

        v_rows = keep.tile([P, R], U8, name="v_rows", align_bytes=64)
        nc.vector.tensor_copy(v_rows[:], v_table_scales[:].indirect(items_sb[:]))
        for q in range(4):
            first = P - 16 + 4 * q
            nc.sync.dma_start(out=v_plane[32 * q : 32 * q + 4].bitcast(I32), in_=v_rows[first : first + 4].bitcast(I32))

        x_plane = keep.tile([P, S], U8, name="x_plane", align_bytes=64)
        nc.vector.tensor_copy(x_plane[:], x_table_scales[:].indirect(offs_sb[:]))

        w_grouped = stage.tile([P, PACK, P, PACK], BF16, name="w_grouped", align_bytes=64, offset=2 * W_BYTES)
        w_codes = keep.tile([P, PACK, P], U32, name="w_codes", align_bytes=64)
        w_plane = keep.tile([P, PACK, P], U8, name="w_plane", tag="x_table_scales", align_bytes=64)
        for raw, first, split in ((w_first, 0, 44), (w_rest, W_FIRST // PACK, 30)):
            groups = raw[:].rearrange("p r (m j) -> p m j r", j=PACK)
            for cast, lo, hi in ((nc.vector.tensor_copy, 0, split), (nc.scalar.copy, split, groups.shape[1])):
                cast(w_grouped[:, :, first + lo : first + hi, :].rearrange("p j m r -> p m j r"), groups[:, lo:hi])
        x_codes = {}

        def gather_x(first, count, offset):
            picked = stage.tile([P, count * P], U32, name="x_codes%d" % first, align_bytes=64, offset=offset)
            entries = offs_sb[:, LIST_COLS * first : LIST_COLS * (first + count)]
            nc.vector.tensor_copy(picked[:], x_table[:].indirect(entries))
            for n in range(count):
                x_codes[first + n] = picked[:, n * P : (n + 1) * P]

        for half in (slice(0, 2), slice(2, 4)):
            if half.start:
                gather_x(1, 1, 10 * W_BYTES)
            nc.vector.quantize_mx(
                out=w_codes[:, half].rearrange("p j m -> p (j m)").bitcast(FP8X4),
                scales=w_plane[:, half].rearrange("p j m -> p (j m)"),
                in_=w_grouped[:, half].rearrange("p j m r -> p (j m r)"),
            )
        gather_x(0, 1, 0)
        gather_x(2, 2, 4 * P)

        bias_picked = stage.tile([P, R], F32, name="bias_picked", align_bytes=64, offset=2 * W_BYTES - 4 * R)
        nc.scalar.activation(bias_picked[:], bias_table[:].indirect(items_sb[:]), ACT.Copy)

        y_ps, sums, others, z_bf, z_mx, others_ps = {}, {}, {}, {}, {}, []
        y_sb = [
            stage.tile([P, D // 2, 2, BASKETS, PACK], F32, name="y_sb%d" % h, align_bytes=64, offset=(6 + h) * W_BYTES // 2)
            for h in range(2)
        ]

        rows = (slice(0, P), slice(P, 3 * P, 2), slice(P + 1, 3 * P, 2), slice(3 * P, 4 * P))

        def project(a):
            y_ps[a] = psum.tile([P, PACK, P], F32, name="y", tag="bank%d" % a)
            for j in range(PACK):
                product(
                    nc, y_ps[a][:, j, :], (w_codes[:, j, :], w_plane[:, j, :]), (x_codes[a], x_plane[:, a * P : (a + 1) * P])
                )

        def copy_out(a, h):
            nc.scalar.copy(y_sb[h][:, :, a - 1], y_ps[a][:].rearrange("p j (v d) -> p d v j", d=D)[:, h::2])

        def add_basket(a, offset, first=0, count=BASKETS):
            if first == 0:
                sums[a, 0] = stage.tile([P, BASKETS, PACK], F32, name="sums%d" % a, align_bytes=64, offset=offset)
            part = slice(first, first + count)
            by_basket = y_ps[a][:].rearrange("p j (v d) -> p v j d", d=D)
            nc.vector.tensor_reduce(sums[a, 0][:, part], by_basket[:, part], mybir.AxisListType.X, ALU.add)

        def leave_out(a, offset, first=0, count=BASKETS):
            if first == 0:
                others[a, 0] = stage.tile([P, BASKETS, D, PACK], F32, name="others%d" % a, align_bytes=64, offset=offset)
            part = slice(first, first + count)
            nc.vector.tensor_tensor(
                others[a, 0][:, part],
                sums[a, 0][:, part].unsqueeze(2).to_broadcast([P, count, D, PACK]),
                y_ps[a][:].rearrange("p j (v d) -> p v d j", d=D)[:, part],
                ALU.subtract,
            )

        def scale_by_norm(a, offset, first=0, count=BASKETS):
            if first == 0:
                z_bf[a] = stage.tile([P, P, PACK], BF16, name="z%d" % a, align_bytes=64, offset=offset)
            entries = slice(first * D, (first + count) * D)
            nc.vector.tensor_tensor(
                z_bf[a][:, entries],
                others[a, first][:].rearrange("p v d j -> p (v d) j"),
                norm_sb[:, a * P : (a + 1) * P][:, entries].unsqueeze(2).to_broadcast([P, count * D, PACK]),
                ALU.mult,
            )

        def item(d):
            return y_sb[d % 2][:, d // 2].rearrange("p s v j -> p (s v j)")

        def negate_items(h, bank):
            items_turned = psum.tile([P, D // 2, P], F32, name="items_turned", tag=bank)
            for n in range(D // 2):
                nc.tensor.transpose(items_turned[:, n, :], item(2 * n + h), ident[:])
            minus_y = stage.tile([P, D // 2, P], F32, name="minus_y%d" % h, align_bytes=64, offset=(7 + h) * W_BYTES)
            nc.scalar.activation(minus_y[:], items_turned[:], ACT.Copy, scale=-1.0)
            return minus_y

        def add_items(bank):
            turned = psum.tile([P, P], F32, name="turned", tag=bank)
            for n in range(D):
                d = 2 * n % D + 2 * n // D
                nc.tensor.matmul(turned[:], lhsT=item(d), rhs=ident[:], start=(n == 0), stop=(n == D - 1), is_transpose=True)
            total = keep.tile([P, P], F32, name="total", align_bytes=64)
            nc.scalar.copy(total[:], turned[:])
            return total

        def turn_back(total, minus_y, bank):
            half = psum.tile([P, D // 2, 2, BASKETS, PACK], F32, name="others_ps", tag=bank)
            terms = [minus_y[:, n, :] for n in range(D // 2)] + [total[:]] * (D // 2)
            for n, term in enumerate(terms):
                nc.tensor.matmul(
                    half[:, n % (D // 2)].rearrange("p s v j -> p (s v j)"),
                    lhsT=term,
                    rhs=ident[:],
                    start=(n == 0),
                    stop=(n == D - 1),
                    is_transpose=True,
                )
            others_ps.append(half)

        def scale_bank(h):
            z_bf[1 + h] = ring.tile([P, P, PACK], BF16, name="z", align_bytes=64)
            factors = norm_sb[:, P : 3 * P].rearrange("p (v d) -> p v d", d=D)[:, :, h::2]
            nc.vector.tensor_tensor(
                z_bf[1 + h][:].rearrange("p (v n) j -> p v n j", n=D // 2),
                others_ps[h][:].rearrange("p n s v j -> p (s v) n j"),
                factors.unsqueeze(3).to_broadcast([P, 2 * BASKETS, D // 2, PACK]),
                ALU.mult,
            )

        def quantize_z(a):
            z_codes = ring.tile([P, P], U32, name="z_codes", align_bytes=64)
            if a == 0:
                z_plane = stage.tile([P, P], U8, name="z_plane0", align_bytes=64, offset=7 * W_BYTES)
            else:
                z_plane = ring.tile([P, P], U8, name="z_plane", align_bytes=64)
            nc.vector.quantize_mx(
                out=z_codes[:].bitcast(FP8X4), scales=z_plane[:], in_=z_bf[a][:].rearrange("p t j -> p (t j)")
            )
            z_mx[a] = (z_codes[:], z_plane[:])

        def score_turned(a, score_bank, blocks=TILES):
            scores = psum.tile([P, blocks, P], F32, name="scores_turned", tag=score_bank)
            for b in range(blocks):
                targets = slice(b * P, (b + 1) * P)
                product(nc, scores[:, b, :], (v_codes[:, targets], v_plane[:, targets]), z_mx[a])
            return scores

        def squash_turned(scores):
            probs = ring.tile([P, TILES, P], F32, name="probs", align_bytes=64)
            for b in range(scores.shape[1]):
                nc.scalar.activation(probs[:, b, :], scores[:, b, :], ACT.Sigmoid, bias=bias_cols[:, b : b + 1])
            return probs

        def finish_turned(a, probs, turn_banks):
            for h, bank in enumerate(turn_banks):
                probs_back = psum.tile([P, 2, P], F32, name="probs_back", tag=bank)
                for n in range(2):
                    nc.tensor.transpose(probs_back[:, n, :], probs[:, 2 * h + n, :], ident[:])
                result = ring.tile([P, HALF], F32, name="result", align_bytes=64)
                nc.scalar.copy(result[:], probs_back[:].rearrange("p b g -> p (b g)"))
                nc.sync.dma_start(out=out[rows[a], h * HALF : (h + 1) * HALF], in_=result[:])

        def score_half(a, h, bank):
            targets = slice(h * HALF, (h + 1) * HALF)
            scores = psum.tile([P, HALF], F32, name="scores_direct", tag=bank)
            product(nc, scores[:], z_mx[a], (v_codes[:, targets], v_plane[:, targets]))
            return scores

        def finish_half(a, h, scores, queue):
            targets = slice(h * HALF, (h + 1) * HALF)
            logits = ring.tile([P, HALF], F32, name="logits", align_bytes=64)
            nc.vector.tensor_tensor(logits[:], scores[:], bias_rows[:, targets], ALU.add)
            result = ring.tile([P, HALF], F32, name="result", align_bytes=64)
            nc.scalar.activation(result[:], logits[:], ACT.Sigmoid)
            queue.dma_start(out=out[rows[a], targets], in_=result[:])

        def score_direct(a, h, bank, queue):
            finish_half(a, h, score_half(a, h, bank), queue)

        project(1)
        first_ps = []
        for bank in ("bank0", "bank5"):
            half = psum.tile([P, 2, P], F32, name="first_ps", tag=bank)
            for n in range(2):
                j = 2 * len(first_ps) + n
                product(nc, half[:, n, :], (w_codes[:, j, :], w_plane[:, j, :]), (x_codes[0], x_plane[:, :P]))
            first_ps.append(half)
        for a in range(2, TILES):
            project(a)
        for a in (1, 2):
            for h in range(2):
                copy_out(a, h)
        first_sums = keep.tile([P, 2, BASKETS, 2], F32, name="first_sums", align_bytes=64)
        first_others = keep.tile([P, 2, BASKETS, D, 2], F32, name="first_others", align_bytes=64)
        for u in range(2):
            nc.vector.tensor_reduce(
                first_sums[:, u], first_ps[u][:].rearrange("p j (v d) -> p v j d", d=D), mybir.AxisListType.X, ALU.add
            )
        for u in range(2):
            nc.vector.tensor_tensor(
                first_others[:, u],
                first_sums[:, u].unsqueeze(2).to_broadcast([P, BASKETS, D, 2]),
                first_ps[u][:].rearrange("p j (v d) -> p v d j", d=D),
                ALU.subtract,
            )
        for first in (0, BASKETS // 2):
            add_basket(3, 13 * W_BYTES, first, BASKETS // 2)
        for first in (0, BASKETS // 2):
            leave_out(3, 12 * W_BYTES, first, BASKETS // 2)
        bias_turned = psum.tile([P, TILES, P], F32, name="bias_turned", tag="bank7")
        for b in range(TILES):
            nc.tensor.transpose(bias_turned[:, b, :], bias_picked[:, b * P : (b + 1) * P], ident[:])
        bias_cols = keep.tile([P, TILES], F32, name="bias_cols")
        nc.scalar.copy(bias_cols[:], bias_turned[:, :, 0])
        minus_even = negate_items(0, "bank1")
        total = add_items("bank4")
        minus_odd = negate_items(1, "bank2")
        v_codes = keep.tile([P, R], U32, name="v_codes", align_bytes=64)
        nc.vector.tensor_copy(v_codes[:], v_table[:].indirect(items_sb[:]))
        z_bf[0] = keep.tile([P, P, PACK], BF16, name="z0", align_bytes=64)
        nc.gpsimd.tensor_tensor(
            z_bf[0][:].rearrange("p t (u j) -> p t u j", u=2),
            first_others[:].rearrange("p u v d j -> p (v d) u j"),
            norm_sb[:, :P].unsqueeze(2).unsqueeze(3).to_broadcast([P, P, 2, 2]),
            ALU.mult,
        )
        turn_back(total, minus_even, "bank5")
        bias_spread = psum.tile([P, TILES, P], F32, name="bias_spread", tag="bank1")
        for b in range(TILES):
            nc.tensor.transpose(bias_spread[:, b, :], bias_cols[:, b : b + 1].to_broadcast([P, P]), ident[:])
        bias_rows = keep.tile([P, R], F32, name="bias_rows", align_bytes=64)
        nc.scalar.copy(bias_rows[:], bias_spread[:].rearrange("p b g -> p (b g)"))
        quantize_z(0)
        scores0 = score_turned(0, "bank0", 2)
        scores0_direct = score_half(0, 1, "bank7")
        turn_back(total, minus_odd, "bank6")
        probs0 = squash_turned(scores0)
        finish_turned(0, probs0, ("bank4",))
        scale_bank(0)
        scale_by_norm(3, 7 * W_BYTES + P)
        quantize_z(1)
        finish_half(0, 1, scores0_direct, nc.sync)
        scale_bank(1)
        quantize_z(3)
        score_direct(1, 0, "bank1", nc.sync)
        quantize_z(2)
        score_direct(1, 1, "bank5", nc.sync)
        score_direct(3, 0, "bank3", nc.sync)
        score_direct(3, 1, "bank0", nc.sync)
        score_direct(2, 0, "bank2", nc.sync)
        score_direct(2, 1, "bank6", nc.scalar)
